import numpy as np
import ml_dtypes


def mxq(x, axis, fmt="e4m3"):
    dtype, down = {"e4m3": (ml_dtypes.float8_e4m3fn, 7), "e5m2": (ml_dtypes.float8_e5m2, 14)}[fmt]
    v = np.moveaxis(np.asarray(x, np.float32).astype(ml_dtypes.bfloat16).astype(np.float64), axis, -1)
    blocks = v.reshape(v.shape[:-1] + (-1, 32))
    amax = np.abs(blocks).max(-1, keepdims=True)
    byte = np.maximum(np.where(amax > 0, np.frexp(amax)[1] - 1 + 127, 0) - down, 1)
    scale = np.exp2(byte - 127.0)
    codes = (blocks / scale).astype(np.float32).astype(dtype).astype(np.float64)
    return np.moveaxis((codes * scale).reshape(v.shape), -1, axis)


WIDE = False


def mx_kscale(k):
    if not WIDE:
        return np.ones(k)
    levels = np.array([10, -10, 5, -5, 0])
    if k % 512:
        return np.exp2(np.random.permutation(np.resize(levels, k // 32))).repeat(32)
    a = np.empty((k // 512, 16))
    for p in range(k // 512):
        a[p, :8] = np.random.permutation(np.resize(levels, 8))
        for g in range(8):
            far = levels[np.abs(levels - a[p, g]) >= 10]
            a[p, g + 8] = far[np.random.randint(len(far))]
    return np.exp2(a.ravel()).repeat(32)


def f64(x):
    return np.asarray(x).astype(np.float64)


def striped(idx):
    return np.tile(idx.reshape(-1, 16).T, (8, 1)).astype(np.uint16)


def unstriped(offs):
    return offs[:16].T.reshape(-1).astype(np.int64)


def striped8(idx):
    return np.concatenate([x.reshape(-1, 16).T for x in idx]).astype(np.uint16)


def runs(offs, k):
    lists = np.stack([offs[16 * r : 16 * r + 16].T.reshape(-1) for r in range(8)]).astype(np.int64)
    return lists[np.arange(k) % 512 // 64]


def pack_weight(w):
    k, n = w.shape
    w = f64(np.asarray(w, np.float32).astype(ml_dtypes.bfloat16)).reshape(k // 32, 32, n)
    amax = np.abs(w).max(1)
    byte = np.clip(np.where(amax > 0, np.frexp(amax)[1] - 1 + 127 - 7, 1), 1, 254)
    scaled = (w * np.exp2(127.0 - byte)[:, None, :]).reshape(k, n).astype(np.float32)
    words = np.ascontiguousarray(scaled.reshape(k // 512, 128, 4, n).transpose(0, 1, 3, 2)).astype(ml_dtypes.float8_e4m3fn).view(np.uint8)
    return words, np.ascontiguousarray(byte.astype(np.uint8).reshape(k // 512, 16, n))


def unpack_weight(words, scales):
    g, p, n, _ = words.shape
    vals = np.ascontiguousarray(words).view(ml_dtypes.float8_e4m3fn).astype(np.float64) * np.repeat(np.exp2(scales.astype(np.float64) - 127.0), 8, axis=1)[..., None]
    return vals.transpose(0, 1, 3, 2).reshape(g * 512, n)


E2M1 = np.array([0.0, 0.5, 1.0, 1.5, 2.0, 3.0, 4.0, 6.0, -0.0, -0.5, -1.0, -1.5, -2.0, -3.0, -4.0, -6.0])


def pack_fp4(w):
    k, n = w.shape
    w = f64(np.asarray(w, np.float32).astype(ml_dtypes.bfloat16)).reshape(k // 32, 32, n)
    amax = np.abs(w).max(1)
    mant, ex = np.frexp(amax / 6.0)
    byte = np.clip(np.where(amax > 0, np.where(mant > 0.5, ex, ex - 1) + 127, 1), 1, 254)
    scaled = (w * np.exp2(127.0 - byte)[:, None, :]).reshape(k, n).astype(np.float32)
    c = np.ascontiguousarray(scaled.reshape(k // 512, 128, 4, n).transpose(0, 1, 3, 2)).astype(ml_dtypes.float4_e2m1fn).view(np.uint8) & 0xF
    words = (c[..., 0::2] | (c[..., 1::2] << 4)).reshape(k // 512, 128, 2 * n)
    return np.ascontiguousarray(words), np.ascontiguousarray(byte.astype(np.uint8).reshape(k // 512, 16, n))


def unpack_fp4(words, scales):
    g, _, n = scales.shape
    words = np.ascontiguousarray(words).reshape(g, 128, n, 2)
    nib = np.empty((g, 128, n, 4), np.uint8)
    nib[..., 0::2] = words & 0xF
    nib[..., 1::2] = words >> 4
    vals = E2M1[nib] * np.repeat(np.exp2(scales.astype(np.float64) - 127.0), 8, axis=1)[..., None]
    return vals.transpose(0, 1, 3, 2).reshape(g * 512, n)


def planes(y):
    n, m = y.shape
    v = y.astype(np.float32).astype(ml_dtypes.bfloat16).astype(np.float64).reshape(n // 32, 32, m)
    top = np.abs(v).max(1)
    byte = np.clip(np.where(top > 0, np.frexp(top)[1] - 1 + 127 - 7, 1), 1, 254)
    codes = (v * np.exp2(127.0 - byte)[:, None, :]).reshape(n, m).astype(np.float32).astype(ml_dtypes.float8_e4m3fn).view(np.uint8)
    words = codes.reshape(n // 512, 128, 4, m).transpose(0, 1, 3, 2)
    return np.ascontiguousarray(words), np.ascontiguousarray(byte.astype(np.uint8).reshape(n // 512, 16, m))


K, T, S, H, J, C = 512, 2048, 512, 512, 512, 512


def setup_inputs():
    n = np.random.standard_normal
    s = mx_kscale(K)[:, None]
    packed_xT = pack_weight(n((K, T)) * s)
    packed_w1 = pack_fp4(n((K, H)) / np.sqrt(K) / s)
    return {
        "x_words": packed_xT[0],
        "x_scales": packed_xT[1],
        "w1_words": packed_w1[0],
        "w1_scales": packed_w1[1],
        "tab": np.random.uniform(0.4, 1.4, (H, J)).astype(np.float32),
        "gs": (np.random.uniform(0.5, 1.5, (K, 1)) / s).astype(np.float32),
        "offs": striped(np.random.permutation(T)[:S]),
        "n1": striped8(np.random.randint(0, J, (8, S))),
        "n2": striped8(np.stack([np.random.permutation(S) for _ in range(8)])),
        "cand": striped(np.random.permutation(T)[:C]),
        "n3": striped8(np.stack([np.random.permutation(S) for _ in range(8)])),
        "n4": striped8(np.stack([np.random.permutation(S) for _ in range(8)])),
    }


def reference(x_words, x_scales, w1_words, w1_scales, tab, gs, offs, n1, n2, cand, n3, n4):
    x_cand = unpack_weight(x_words, x_scales)[:, unstriped(cand)]
    xq = unpack_weight(x_words, x_scales)[:, unstriped(offs)]
    y = unpack_fp4(w1_words, w1_scales).T @ xq
    z = f64(gs) * (y * (f64(tab)[np.arange(H)[:, None], runs(n1, H)]) - (0.5 * (y[np.arange(H)[:, None], runs(n2, H)])))
    s = 0.0625 * ((x_cand.T @ mxq(z, 0, "e4m3")))
    pa = s[np.arange(C)[:, None], runs(n3, C)]
    kr = np.exp(-0.5 * ((s - pa) ** 2))
    pb = s[np.arange(C)[:, None], runs(n4, C)]
    kr2 = np.exp(-0.5 * ((s - pb) ** 2))
    out_0 = (kr * pa + kr2 * pb) / (kr + kr2 + 0.5)
    return (out_0,) + planes(out_0)

@@ -1,0 +1,226 @@
+from contextlib import ExitStack
+
+import concourse.mybir as mybir
+from concourse.masks import make_identity
+
+K, T, S = 512, 2048, 512
+FLOPS = 2 * 2 * 512 * 512 * 512
+
+F32 = mybir.dt.float32
+BF16 = mybir.dt.bfloat16
+I32 = mybir.dt.int32
+U32 = mybir.dt.uint32
+U16 = mybir.dt.uint16
+U8 = mybir.dt.uint8
+FP8X4 = mybir.dt.float8_e4m3fn_x4
+FP4X4 = mybir.dt.float4_e2m1fn_x4
+ACT = mybir.ActivationFunctionType
+ALU = mybir.AluOpType
+
+P = 128
+PACK = 4
+UNIT = 128
+UNITS = S // UNIT
+Z_PIECES = ((0, 256), (256, 128), (384, 128))
+
+
+def entries(lst, start, count):
+    return lst[:, start // 16 : (start + count) // 16]
+
+
+def interleave(copy, dst, src):
+    copy(dst.rearrange("p (c i) t -> p c t i", i=4), src.rearrange("p t (c i) -> p c t i", i=4))
+
+
+def tile_picked_candkindgkern_none_po_kernel(
+    tc, x_words, x_scales, w1_words, w1_scales, tab, gs, offs, n1, n2, cand, n3, n4, out_0, out_1, out_2
+):
+    nc = tc.nc
+    with ExitStack() as ctx:
+        lists = ctx.enter_context(tc.tile_pool(name="lists", bufs=1))
+        sb = ctx.enter_context(tc.tile_pool(name="sb", bufs=1))
+        psum = ctx.enter_context(tc.psum_pool(name="psum", bufs=1))
+
+        def sbuf(name, shape, dtype):
+            return sb.tile(shape, dtype, name=name, align_bytes=64)
+
+        def bank(b, name, shape):
+            return psum.tile(shape, F32, name=name, tag="bank%d" % b)
+
+        def load_list(name, src):
+            lst = lists.tile([P, S // 16], U16, name=name)
+            nc.sync.dma_start(lst[:], src)
+            return lst
+
+        xs = sbuf("xs", [P, T], U8)
+        nc.vector.memset(xs[:].bitcast(I32), 0)
+        ws = sb.tile([P, S], U8, name="ws", tag="ws_then_cand", align_bytes=64)
+        nc.gpsimd.memset(ws[:].bitcast(I32), 0)
+        offs_l = load_list("offs_l", offs)
+        xw = sbuf("xw", [P, T], I32)
+        nc.scalar.dma_start(xw[:], x_words[0].rearrange("p n t -> p (n t)").bitcast(I32))
+        cand_l = load_list("cand_l", cand)
+        ww = sbuf("ww", [P, 2 * S], U8)
+        nc.sync.dma_start(ww[:].bitcast(I32), w1_words[0].bitcast(I32))
+        for q in range(4):
+            nc.sync.dma_start(xs[32 * q : 32 * q + 4, :].bitcast(I32), x_scales[0, 4 * q : 4 * q + 4, :].bitcast(I32))
+        for q in range(4):
+            (nc.gpsimd if q < 3 else nc.sync).dma_start(ws[32 * q : 32 * q + 4, :].bitcast(I32), w1_scales[0, 4 * q : 4 * q + 4, :].bitcast(I32))
+        gain = sbuf("gain", [P, PACK], F32)
+        nc.sync.dma_start(gain[:], gs.rearrange("(p t) o -> p (t o)", t=PACK))
+        n1_l = load_list("n1_l", n1)
+        tab_rows = tab.rearrange("(p t) c -> p t c", t=PACK)
+        tabs = [sbuf("tab%d" % t, [P, S], F32) for t in range(PACK)]
+        nc.sync.dma_start(tabs[0][:], tab_rows[:, 0, :])
+        n2_l = load_list("n2_l", n2)
+        for t in range(1, PACK):
+            nc.sync.dma_start(tabs[t][:], tab_rows[:, t, :])
+        n3_l = load_list("n3_l", n3)
+        n4_l = load_list("n4_l", n4)
+        ident = sbuf("ident", [P, P], F32)
+        make_identity(nc, ident[:])
+        half_gain = sbuf("half_gain", [P, PACK], F32)
+        nc.scalar.activation(half_gain[:], gain[:], ACT.Copy, scale=-0.5)
+
+        tok_s = sbuf("tok_s", [P, S], U8)
+        nc.vector.tensor_copy(tok_s[:], xs[:].indirect(offs_l[:]))
+        ww_d = sbuf("ww_d", [P, 2 * S], U8)
+        nc.vector.tensor_copy(
+            ww_d[:].rearrange("p (t m b) -> p t m b", t=PACK, b=2), ww[:].rearrange("p (m t b) -> p t m b", t=PACK, b=2)
+        )
+        ws_d = sbuf("ws_d", [P, S], U8)
+        nc.vector.tensor_copy(ws_d[:].rearrange("p (t m) -> p t m", t=PACK), ws[:].rearrange("p (m t) -> p t m", t=PACK))
+        tok_w = sbuf("tok_w", [P, S], U32)
+        nc.vector.tensor_copy(tok_w[:], xw[:].bitcast(U32).indirect(offs_l[:]))
+        cand_w = sb.tile([P, S], U32, name="cand_w", tag="ws_then_cand", align_bytes=64)
+        nc.vector.tensor_copy(cand_w[:].rearrange("p (t m) -> p m t", t=PACK), xw[:].bitcast(U32).indirect(cand_l[:]))
+        cand_s = sbuf("cand_s", [P, S], U8)
+        nc.vector.tensor_copy(cand_s[:], xs[:].indirect(cand_l[:]))
+        cand_sd = sbuf("cand_sd", [P, S], U8)
+        nc.vector.tensor_copy(
+            cand_sd[:].rearrange("p (t m) -> p t m", t=PACK), cand_s[:].rearrange("p (m t) -> p t m", t=PACK)
+        )
+
+        gy = [sbuf("gy%d" % t, [P, S], F32) for t in range(PACK)]
+        hy = [sbuf("hy%d" % t, [P, S], F32) for t in range(PACK)]
+        for t in range(PACK):
+            y = bank(t, "y%d" % t, [P, S])
+            nc.tensor.matmul_mx(
+                out=y[:],
+                lhsT=ww_d[:, 2 * P * t : 2 * P * (t + 1)].bitcast(FP4X4),
+                lhsT_scale=ws_d[:, P * t : P * (t + 1)],
+                rhs=tok_w[:].bitcast(FP8X4),
+                rhs_scale=tok_s[:],
+                start=True,
+                stop=True,
+            )
+            nc.scalar.activation(gy[t][:], y[:], ACT.Copy, scale=gain[:, t : t + 1])
+            nc.scalar.activation(hy[t][:], y[:], ACT.Copy, scale=half_gain[:, t : t + 1])
+
+        score = [sbuf("score%d" % t, [P, S], F32) for t in range(PACK)]
+        neg = [sbuf("neg%d" % c, [P, PACK, UNIT], F32) for c in range(UNITS)]
+        for piece, (start, n) in enumerate(Z_PIECES):
+            prod = [sbuf("prod%d_%d" % (start, t), [P, n], F32) for t in range(PACK - 1)]
+            prod.append(sb.tile([P, n], F32, name="prod_last%d" % piece, tag="rounded%d" % ((piece - 1) % len(Z_PIECES)), align_bytes=64))
+            z = sbuf("z%d" % start, [P, PACK, n], F32)
+            for t in range(PACK + 1):
+                if t < PACK:
+                    nc.vector.tensor_tensor(
+                        prod[t][:], tabs[t][:].indirect(entries(n1_l, start, n)), gy[t][:, start : start + n], ALU.mult
+                    )
+                if t > 0:
+                    nc.vector.tensor_tensor(
+                        z[:, t - 1, :], hy[t - 1][:].indirect(entries(n2_l, start, n)), prod[t - 1][:], ALU.add
+                    )
+            zb = sb.tile([P, n, PACK], BF16, name="zb%d" % piece, tag="rounded%d" % piece, align_bytes=64)
+            interleave(nc.vector.tensor_copy if start + n == S else nc.scalar.copy, zb[:], z[:])
+            z_w = sbuf("z_w%d" % start, [P, n], U32)
+            z_s = sbuf("z_s%d" % start, [P, n], U8)
+            nc.vector.quantize_mx(out=z_w[:].bitcast(FP8X4), scales=z_s[:], in_=zb[:].rearrange("p n t -> p (n t)"))
+            for lo in range(0, n, UNIT):
+                c = (start + lo) // UNIT
+                raw = bank(4 + c, "raw%d" % c, [P, PACK, UNIT])
+                for t in range(PACK):
+                    nc.tensor.matmul_mx(
+                        out=raw[:, t, :],
+                        lhsT=cand_w[:, P * t : P * (t + 1)].bitcast(FP8X4),
+                        lhsT_scale=cand_sd[:, P * t : P * (t + 1)],
+                        rhs=z_w[:, lo : lo + UNIT].bitcast(FP8X4),
+                        rhs_scale=z_s[:, lo : lo + UNIT],
+                        start=True,
+                        stop=True,
+                    )
+                for t in range(PACK):
+                    nc.scalar.activation(score[t][:, c * UNIT : (c + 1) * UNIT], raw[:, t, :], ACT.Copy, scale=0.0625)
+                nc.scalar.activation(neg[c][:], raw[:], ACT.Copy, scale=-0.0625)
+
+        def add_transposed(dst, src, first, last):
+            for t in range(PACK):
+                nc.tensor.matmul(
+                    dst[:, t, :], src[:, t, :], ident[:], start=first and t == 0, stop=last and t == PACK - 1, is_transpose=True
+                )
+
+        root = sbuf("root", [P, UNITS, PACK * UNIT], F32)
+        num = [bank(c, "num%d" % c, [P, PACK, UNIT]) for c in range(UNITS)]
+        wsum = [bank(4 + c, "wsum%d" % c, [P, PACK, UNIT]) for c in range(UNITS)]
+        diff, weight = {}, {}
+        for c in range(UNITS):
+            add_transposed(num[c], neg[c], True, False)
+        for c in range(UNITS):
+            for j, lst in enumerate((n3_l, n4_l)):
+                d = sbuf("diff%d_%d" % (c, j), [P, PACK, UNIT], F32)
+                for t in range(PACK):
+                    nc.vector.tensor_tensor(
+                        d[:, t, :], score[t][:].indirect(entries(lst, c * UNIT, UNIT)), neg[c][:, t, :], ALU.add
+                    )
+                if (c, j) == (UNITS - 1, 1):
+                    sq = root[:, :, 0:UNIT]
+                else:
+                    sq = sbuf("sq%d_%d" % (c, j), [P, PACK, UNIT], F32)[:]
+                nc.scalar.activation(sq, d[:], ACT.Square)
+                e = sbuf("weight%d_%d" % (c, j), [P, PACK, UNIT], F32)
+                nc.scalar.activation(e[:], sq, ACT.Exp, scale=-0.5)
+                add_transposed(wsum[c], e, j == 0, j == 1)
+                diff[c, j], weight[c, j] = d, e
+        for c in range(UNITS):
+            for j in range(2):
+                pull = sbuf("pull%d_%d" % (c, j), [P, PACK, UNIT], F32)
+                nc.vector.scalar_tensor_tensor(
+                    pull[:].rearrange("p t n -> p (t n)"),
+                    weight[c, j][:].rearrange("p t n -> p (t n)"),
+                    2.0,
+                    diff[c, j][:].rearrange("p t n -> p (t n)"),
+                    ALU.mult,
+                    ALU.mult,
+                )
+                add_transposed(num[c], pull, False, j == 1)
+
+        out_rows = out_0.rearrange("(p t) j -> p t j", t=PACK)
+        words_out = out_1[0].rearrange("p n t -> p (n t)").bitcast(I32)
+        o_w = sbuf("o_w", [P, S], U32)
+        o_s = sbuf("o_s", [P, S], U8)
+        recip = [sbuf("recip%d" % c, [P, PACK * UNIT], F32) for c in range(UNITS)]
+        for c in range(UNITS):
+            nc.scalar.activation(
+                root[:, c, :], wsum[c][:].rearrange("p t n -> p (t n)"), ACT.Ln, scale=2.0, bias=1.0
+            )
+        for c in range(UNITS):
+            nc.scalar.activation(recip[c][:], root[:, c, :], ACT.Exp, scale=-1.0)
+        for c in range(UNITS):
+            cols = slice(c * UNIT, (c + 1) * UNIT)
+            shift = sbuf("shift%d" % c, [P, PACK, UNIT], F32)
+            nc.vector.tensor_tensor(
+                shift[:].rearrange("p t n -> p (t n)"), num[c][:].rearrange("p t n -> p (t n)"), recip[c][:], ALU.mult
+            )
+            back = bank(4 + c, "back%d" % c, [P, PACK, UNIT])
+            add_transposed(back, shift, True, True)
+            res = sbuf("res%d" % c, [P, PACK, UNIT], F32)
+            nc.vector.tensor_tensor(res[:], back[:], neg[c][:], ALU.subtract)
+            nc.sync.dma_start(out_rows[:, :, cols], res[:])
+            rb = sbuf("rb%d" % c, [P, UNIT, PACK], BF16)
+            interleave(nc.vector.tensor_copy if c == UNITS - 1 else nc.scalar.copy, rb[:], res[:])
+            nc.vector.quantize_mx(out=o_w[:, cols].bitcast(FP8X4), scales=o_s[:, cols], in_=rb[:].rearrange("p n t -> p (n t)"))
+            nc.sync.dma_start(words_out[:, cols], o_w[:, cols].bitcast(I32))
+        for q in range(4):
+            eng = nc.scalar if q % 2 else nc.sync
+            eng.dma_start(out_2[0, 4 * q : 4 * q + 4, :].bitcast(I32), o_s[32 * q : 32 * q + 4, :].bitcast(I32))

@@ -21,7 +21,8 @@ P = 128
 PACK = 4
 UNIT = 128
 UNITS = S // UNIT
-Z_PIECES = ((0, 256), (256, 128), (384, 128))
+HALF = S // 2
+VECTOR_SQUARES = (5,)
 
 
 def entries(lst, start, count):
@@ -53,17 +54,17 @@ def tile_picked_candkindgkern_none_po_kernel(
             return lst
 
         xs = sbuf("xs", [P, T], U8)
-        nc.vector.memset(xs[:].bitcast(I32), 0)
+        nc.gpsimd.memset(xs[:].bitcast(I32), 0)
         ws = sb.tile([P, S], U8, name="ws", tag="ws_then_cand", align_bytes=64)
         nc.gpsimd.memset(ws[:].bitcast(I32), 0)
-        offs_l = load_list("offs_l", offs)
-        xw = sbuf("xw", [P, T], I32)
-        nc.scalar.dma_start(xw[:], x_words[0].rearrange("p n t -> p (n t)").bitcast(I32))
-        cand_l = load_list("cand_l", cand)
         ww = sbuf("ww", [P, 2 * S], U8)
         nc.sync.dma_start(ww[:].bitcast(I32), w1_words[0].bitcast(I32))
+        offs_l = load_list("offs_l", offs)
         for q in range(4):
             nc.sync.dma_start(xs[32 * q : 32 * q + 4, :].bitcast(I32), x_scales[0, 4 * q : 4 * q + 4, :].bitcast(I32))
+        cand_l = load_list("cand_l", cand)
+        xw = sbuf("xw", [P, T], I32)
+        nc.sync.dma_start(xw[:], x_words[0].rearrange("p n t -> p (n t)").bitcast(I32))
         for q in range(4):
             (nc.gpsimd if q < 3 else nc.sync).dma_start(ws[32 * q : 32 * q + 4, :].bitcast(I32), w1_scales[0, 4 * q : 4 * q + 4, :].bitcast(I32))
         gain = sbuf("gain", [P, PACK], F32)
@@ -82,11 +83,17 @@ def tile_picked_candkindgkern_none_po_kernel(
         half_gain = sbuf("half_gain", [P, PACK], F32)
         nc.scalar.activation(half_gain[:], gain[:], ACT.Copy, scale=-0.5)
 
-        tok_s = sbuf("tok_s", [P, S], U8)
-        nc.vector.tensor_copy(tok_s[:], xs[:].indirect(offs_l[:]))
         ww_d = sbuf("ww_d", [P, 2 * S], U8)
         nc.vector.tensor_copy(
             ww_d[:].rearrange("p (t m b) -> p t m b", t=PACK, b=2), ww[:].rearrange("p (m t b) -> p t m b", t=PACK, b=2)
+        )
+        tok_s = sbuf("tok_s", [P, S], U8)
+        nc.vector.tensor_copy(tok_s[:], xs[:].indirect(offs_l[:]))
+        cand_s = sbuf("cand_s", [P, S], U8)
+        nc.vector.tensor_copy(cand_s[:], xs[:].indirect(cand_l[:]))
+        cand_sd = sbuf("cand_sd", [P, S], U8)
+        nc.vector.tensor_copy(
+            cand_sd[:].rearrange("p (t m) -> p t m", t=PACK), cand_s[:].rearrange("p (m t) -> p t m", t=PACK)
         )
         ws_d = sbuf("ws_d", [P, S], U8)
         nc.vector.tensor_copy(ws_d[:].rearrange("p (t m) -> p t m", t=PACK), ws[:].rearrange("p (m t) -> p t m", t=PACK))
@@ -94,19 +101,15 @@ def tile_picked_candkindgkern_none_po_kernel(
         nc.vector.tensor_copy(tok_w[:], xw[:].bitcast(U32).indirect(offs_l[:]))
         cand_w = sb.tile([P, S], U32, name="cand_w", tag="ws_then_cand", align_bytes=64)
         nc.vector.tensor_copy(cand_w[:].rearrange("p (t m) -> p m t", t=PACK), xw[:].bitcast(U32).indirect(cand_l[:]))
-        cand_s = sbuf("cand_s", [P, S], U8)
-        nc.vector.tensor_copy(cand_s[:], xs[:].indirect(cand_l[:]))
-        cand_sd = sbuf("cand_sd", [P, S], U8)
-        nc.vector.tensor_copy(
-            cand_sd[:].rearrange("p (t m) -> p t m", t=PACK), cand_s[:].rearrange("p (m t) -> p t m", t=PACK)
-        )
 
-        gy = [sbuf("gy%d" % t, [P, S], F32) for t in range(PACK)]
-        hy = [sbuf("hy%d" % t, [P, S], F32) for t in range(PACK)]
+        tab2 = [sbuf("tab2_%d" % t, [P, S], F32) for t in range(PACK)]
         for t in range(PACK):
-            y = bank(t, "y%d" % t, [P, S])
+            nc.scalar.activation(tab2[t][:], tabs[t][:], ACT.Copy, scale=2.0)
+        hy = [sbuf("hy%d" % t, [P, S], F32) for t in range(PACK)]
+        ys = [bank(t, "y%d" % t, [P, S]) for t in range(PACK)]
+        for t in range(PACK):
             nc.tensor.matmul_mx(
-                out=y[:],
+                out=ys[t][:],
                 lhsT=ww_d[:, 2 * P * t : 2 * P * (t + 1)].bitcast(FP4X4),
                 lhsT_scale=ws_d[:, P * t : P * (t + 1)],
                 rhs=tok_w[:].bitcast(FP8X4),
@@ -114,86 +117,179 @@ def tile_picked_candkindgkern_none_po_kernel(
                 start=True,
                 stop=True,
             )
-            nc.scalar.activation(gy[t][:], y[:], ACT.Copy, scale=gain[:, t : t + 1])
-            nc.scalar.activation(hy[t][:], y[:], ACT.Copy, scale=half_gain[:, t : t + 1])
+        for t in range(PACK + 1):
+            if t < PACK:
+                nc.scalar.activation(hy[t][:, 0:HALF], ys[t][:, 0:HALF], ACT.Copy, scale=half_gain[:, t : t + 1])
+            if t > 0:
+                nc.scalar.activation(hy[t - 1][:, HALF:S], ys[t - 1][:, HALF:S], ACT.Copy, scale=half_gain[:, t - 1 : t])
 
         score = [sbuf("score%d" % t, [P, S], F32) for t in range(PACK)]
-        neg = [sbuf("neg%d" % c, [P, PACK, UNIT], F32) for c in range(UNITS)]
-        for piece, (start, n) in enumerate(Z_PIECES):
-            prod = [sbuf("prod%d_%d" % (start, t), [P, n], F32) for t in range(PACK - 1)]
-            prod.append(sb.tile([P, n], F32, name="prod_last%d" % piece, tag="rounded%d" % ((piece - 1) % len(Z_PIECES)), align_bytes=64))
-            z = sbuf("z%d" % start, [P, PACK, n], F32)
-            for t in range(PACK + 1):
-                if t < PACK:
-                    nc.vector.tensor_tensor(
-                        prod[t][:], tabs[t][:].indirect(entries(n1_l, start, n)), gy[t][:, start : start + n], ALU.mult
-                    )
-                if t > 0:
-                    nc.vector.tensor_tensor(
-                        z[:, t - 1, :], hy[t - 1][:].indirect(entries(n2_l, start, n)), prod[t - 1][:], ALU.add
-                    )
-            zb = sb.tile([P, n, PACK], BF16, name="zb%d" % piece, tag="rounded%d" % piece, align_bytes=64)
-            interleave(nc.vector.tensor_copy if start + n == S else nc.scalar.copy, zb[:], z[:])
-            z_w = sbuf("z_w%d" % start, [P, n], U32)
-            z_s = sbuf("z_s%d" % start, [P, n], U8)
-            nc.vector.quantize_mx(out=z_w[:].bitcast(FP8X4), scales=z_s[:], in_=zb[:].rearrange("p n t -> p (n t)"))
-            for lo in range(0, n, UNIT):
-                c = (start + lo) // UNIT
-                raw = bank(4 + c, "raw%d" % c, [P, PACK, UNIT])
-                for t in range(PACK):
-                    nc.tensor.matmul_mx(
-                        out=raw[:, t, :],
-                        lhsT=cand_w[:, P * t : P * (t + 1)].bitcast(FP8X4),
-                        lhsT_scale=cand_sd[:, P * t : P * (t + 1)],
-                        rhs=z_w[:, lo : lo + UNIT].bitcast(FP8X4),
-                        rhs_scale=z_s[:, lo : lo + UNIT],
-                        start=True,
-                        stop=True,
-                    )
-                for t in range(PACK):
-                    nc.scalar.activation(score[t][:, c * UNIT : (c + 1) * UNIT], raw[:, t, :], ACT.Copy, scale=0.0625)
-                nc.scalar.activation(neg[c][:], raw[:], ACT.Copy, scale=-0.0625)
+        neg = [sbuf("neg%d" % h, [P, PACK, HALF], F32) for h in range(2)]
 
-        def add_transposed(dst, src, first, last):
-            for t in range(PACK):
+        def neg_unit(c):
+            return neg[c // 2][:, :, (c % 2) * UNIT : (c % 2 + 1) * UNIT]
+
+        def quantised(name, z, n, copy, tag):
+            zb = sb.tile([P, n, PACK], BF16, name="zb" + name, tag=tag, align_bytes=64)
+            interleave(copy, zb[:], z[:])
+            z_w = sbuf("z_w" + name, [P, n], U32)
+            z_s = sbuf("z_s" + name, [P, n], U8)
+            nc.vector.quantize_mx(out=z_w[:].bitcast(FP8X4), scales=z_s[:], in_=zb[:].rearrange("p n t -> p (n t)"))
+            return z_w, z_s
+
+        def second_product(dst, t, zq, start, n):
+            nc.tensor.matmul_mx(
+                out=dst,
+                lhsT=cand_w[:, P * t : P * (t + 1)].bitcast(FP8X4),
+                lhsT_scale=cand_sd[:, P * t : P * (t + 1)],
+                rhs=zq[0][:].bitcast(FP8X4),
+                rhs_scale=zq[1][:],
+                start=True,
+                stop=True,
+            )
+
+        def keep_scores(src, t, start, n):
+            nc.scalar.activation(score[t][:, start : start + n], src, ACT.Copy, scale=0.0625)
+
+        def add_transposed(dst, src, ts, first, last):
+            for t in ts:
                 nc.tensor.matmul(
                     dst[:, t, :], src[:, t, :], ident[:], start=first and t == 0, stop=last and t == PACK - 1, is_transpose=True
                 )
 
+        def unit_of(tile, i):
+            return tile[:, :, i * UNIT : (i + 1) * UNIT]
+
+        every = range(PACK)
+        num, turned = [], []
+
+        def turn_scores(c, tag):
+            tmp = bank(c, "neg_turned%d" % c, [P, PACK, UNIT])
+            add_transposed(tmp, neg_unit(c), every, True, True)
+            turned.append(sb.tile([P, PACK, UNIT], F32, name="turned%d" % c, tag=tag, align_bytes=64))
+            nc.vector.tensor_scalar_mul(turned[c][:], tmp[:], -1.0)
+            acc = bank(c, "num%d" % c, [P, PACK, UNIT])
+            add_transposed(acc, neg_unit(c), every, True, False)
+            num.append(acc)
+
+        def scaled_by_tab(prod, t, start):
+            nc.vector.tensor_tensor(
+                prod, tab2[t][:].indirect(entries(n1_l, start, HALF)), hy[t][:, start : start + HALF], ALU.mult
+            )
+
+        def less_neighbour(z, t, prod, lo, start, n):
+            nc.vector.tensor_tensor(z[:, t, :], hy[t][:].indirect(entries(n2_l, start, n)), prod[:, lo : lo + n], ALU.subtract)
+
+        first_prod = sb.tile([P, PACK, HALF], F32, name="first_prod", tag="prod", align_bytes=64)
+        prod = [first_prod[:, t, :] for t in range(PACK)]
+        z = sbuf("z0", [P, PACK, HALF], F32)
+        for t in range(PACK + 1):
+            if t < PACK:
+                scaled_by_tab(prod[t], t, 0)
+            if t > 0:
+                less_neighbour(z, t - 1, prod[t - 1], 0, 0, HALF)
+        zq = quantised("0", z, HALF, nc.scalar.copy, "rounded")
+        second_prod = sb.tile([P, PACK - 1, HALF], F32, name="second_prod", tag="prod", align_bytes=64)
+        last_prod = sb.tile([P, HALF], F32, name="last_prod", tag="rounded", align_bytes=64)
+        prod = [second_prod[:, t, :] for t in range(PACK - 1)] + [last_prod[:]]
+        for t in range(PACK):
+            scaled_by_tab(prod[t], t, HALF)
+        raw = [bank(4 + b, "raw%d" % b, [P, 2, HALF]) for b in range(2)]
+        for t in range(PACK):
+            second_product(raw[t // 2][:, t % 2, :], t, zq, 0, HALF)
+        for t in range(PACK):
+            keep_scores(raw[t // 2][:, t % 2, :], t, 0, HALF)
+        nc.scalar.activation(neg[0][:, 0:2, :], raw[0][:], ACT.Copy, scale=-0.0625)
+        zs = [sbuf("z%d" % c, [P, PACK, UNIT], F32) for c in (2, 3)]
+        for i in range(2):
+            for t in range(PACK):
+                less_neighbour(zs[i], t, prod[t], i * UNIT, HALF + i * UNIT, UNIT)
+        zq2 = quantised("2", zs[0], UNIT, nc.scalar.copy, "zb2")
+        nc.scalar.activation(neg[0][:, 2:4, :], raw[1][:], ACT.Copy, scale=-0.0625)
+        zq3 = quantised("3", zs[1], UNIT, nc.vector.tensor_copy, "zb3")
+        turn_scores(0, "zb3")
+        for c, zq in ((2, zq2), (3, zq3)):
+            late = bank(4 + c, "raw%d" % c, [P, PACK, UNIT])
+            for t in range(PACK):
+                second_product(late[:, t, :], t, zq, c * UNIT, UNIT)
+            for t in range(PACK):
+                keep_scores(late[:, t, :], t, c * UNIT, UNIT)
+            if c == 2:
+                nc.vector.tensor_scalar_mul(neg_unit(c), late[:], -0.0625)
+            else:
+                nc.scalar.activation(neg_unit(c), late[:], ACT.Copy, scale=-0.0625)
+
         root = sbuf("root", [P, UNITS, PACK * UNIT], F32)
-        num = [bank(c, "num%d" % c, [P, PACK, UNIT]) for c in range(UNITS)]
         wsum = [bank(4 + c, "wsum%d" % c, [P, PACK, UNIT]) for c in range(UNITS)]
         diff, weight = {}, {}
-        for c in range(UNITS):
-            add_transposed(num[c], neg[c], True, False)
-        for c in range(UNITS):
-            for j, lst in enumerate((n3_l, n4_l)):
-                d = sbuf("diff%d_%d" % (c, j), [P, PACK, UNIT], F32)
-                for t in range(PACK):
-                    nc.vector.tensor_tensor(
-                        d[:, t, :], score[t][:].indirect(entries(lst, c * UNIT, UNIT)), neg[c][:, t, :], ALU.add
-                    )
-                if (c, j) == (UNITS - 1, 1):
-                    sq = root[:, :, 0:UNIT]
-                else:
-                    sq = sbuf("sq%d_%d" % (c, j), [P, PACK, UNIT], F32)[:]
-                nc.scalar.activation(sq, d[:], ACT.Square)
-                e = sbuf("weight%d_%d" % (c, j), [P, PACK, UNIT], F32)
-                nc.scalar.activation(e[:], sq, ACT.Exp, scale=-0.5)
-                add_transposed(wsum[c], e, j == 0, j == 1)
-                diff[c, j], weight[c, j] = d, e
-        for c in range(UNITS):
+        steps = []
+        for h in range(2):
             for j in range(2):
-                pull = sbuf("pull%d_%d" % (c, j), [P, PACK, UNIT], F32)
+                diff[h, j] = sbuf("diff%d_%d" % (h, j), [P, PACK, HALF], F32)
+                weight[h, j] = sbuf("weight%d_%d" % (h, j), [P, PACK, HALF], F32)
+                groups = ((0, 1), (2,), (3,)) if (h, j) == (1, 1) else ((0, 1), (2, 3))
+                steps.extend((h, j, ts) for ts in groups)
+
+        def fetch(h, j, t):
+            nc.vector.tensor_tensor(
+                diff[h, j][:, t, :],
+                score[t][:].indirect(entries((n3_l, n4_l)[j], h * HALF, HALF)),
+                neg[h][:, t, :],
+                ALU.add,
+            )
+
+        def rows_of(tile, ts):
+            flat = tile[:, ts[0] : ts[-1] + 1, :].rearrange("p t n -> p (t n)")
+            return flat.rearrange("p (a b) -> p a b", a=UNITS)
+
+        squares = []
+
+        def square(k):
+            h, j, ts = steps[k]
+            if k == len(steps) - 1:
+                sq = root[:, :, 0 : HALF // UNITS]
+            else:
+                sq = sb.tile([P, UNITS, len(ts) * HALF // UNITS], F32, name="sq%d" % k, tag="sq%d" % k, align_bytes=64)[:]
+            d = rows_of(diff[h, j], ts)
+            if k in VECTOR_SQUARES:
+                nc.vector.tensor_tensor(sq, d, d, ALU.mult)
+            else:
+                nc.scalar.activation(sq, d, ACT.Square)
+            squares.append(sq)
+
+        def weigh(k):
+            h, j, ts = steps[k]
+            nc.scalar.activation(rows_of(weight[h, j], ts), squares[k], ACT.Exp, scale=-0.5)
+            for i in range(2):
+                add_transposed(wsum[2 * h + i], unit_of(weight[h, j], i), ts, j == 0, j == 1)
+
+        for k, (h, j, ts) in enumerate(steps):
+            fetch(h, j, ts[0])
+            if k > 0:
+                square(k - 1)
+            if k > 1:
+                weigh(k - 2)
+            for t in ts[1:]:
+                fetch(h, j, t)
+        square(len(steps) - 1)
+        weigh(len(steps) - 2)
+        weigh(len(steps) - 1)
+        for c in range(1, UNITS):
+            turn_scores(c, "sq%d" % (c + 2))
+        pulls = sb.tile([P, 4, PACK, HALF], F32, name="pulls", tag="sq6", align_bytes=64)
+        for h in range(2):
+            for j in range(2):
+                pull = pulls[:, 2 * h + j, :, :]
                 nc.vector.scalar_tensor_tensor(
-                    pull[:].rearrange("p t n -> p (t n)"),
-                    weight[c, j][:].rearrange("p t n -> p (t n)"),
+                    pull.rearrange("p t n -> p (t n)"),
+                    weight[h, j][:].rearrange("p t n -> p (t n)"),
                     2.0,
-                    diff[c, j][:].rearrange("p t n -> p (t n)"),
+                    diff[h, j][:].rearrange("p t n -> p (t n)"),
                     ALU.mult,
                     ALU.mult,
                 )
-                add_transposed(num[c], pull, False, j == 1)
+                for i in range(2):
+                    add_transposed(num[2 * h + i], unit_of(pull, i), every, False, j == 1)
 
         out_rows = out_0.rearrange("(p t) j -> p t j", t=PACK)
         words_out = out_1[0].rearrange("p n t -> p (n t)").bitcast(I32)
@@ -206,19 +302,22 @@ def tile_picked_candkindgkern_none_po_kernel(
             )
         for c in range(UNITS):
             nc.scalar.activation(recip[c][:], root[:, c, :], ACT.Exp, scale=-1.0)
+        back = [bank(4 + c, "back%d" % c, [P, PACK, UNIT]) for c in range(UNITS)]
         for c in range(UNITS):
-            cols = slice(c * UNIT, (c + 1) * UNIT)
+            add_transposed(back[c], turned[c], every, True, False)
+        for c in range(UNITS):
             shift = sbuf("shift%d" % c, [P, PACK, UNIT], F32)
             nc.vector.tensor_tensor(
                 shift[:].rearrange("p t n -> p (t n)"), num[c][:].rearrange("p t n -> p (t n)"), recip[c][:], ALU.mult
             )
-            back = bank(4 + c, "back%d" % c, [P, PACK, UNIT])
-            add_transposed(back, shift, True, True)
+            add_transposed(back[c], shift, every, False, True)
+        for c in range(UNITS):
+            cols = slice(c * UNIT, (c + 1) * UNIT)
             res = sbuf("res%d" % c, [P, PACK, UNIT], F32)
-            nc.vector.tensor_tensor(res[:], back[:], neg[c][:], ALU.subtract)
-            nc.sync.dma_start(out_rows[:, :, cols], res[:])
             rb = sbuf("rb%d" % c, [P, UNIT, PACK], BF16)
-            interleave(nc.vector.tensor_copy if c == UNITS - 1 else nc.scalar.copy, rb[:], res[:])
+            nc.scalar.copy(res[:], back[c][:])
+            nc.sync.dma_start(out_rows[:, :, cols], res[:])
+            interleave(nc.vector.tensor_copy, rb[:], res[:])
             nc.vector.quantize_mx(out=o_w[:, cols].bitcast(FP8X4), scales=o_s[:, cols], in_=rb[:].rearrange("p n t -> p (n t)"))
             nc.sync.dma_start(words_out[:, cols], o_w[:, cols].bitcast(I32))
         for q in range(4):

@@ -22,7 +22,6 @@ PACK = 4
 UNIT = 128
 UNITS = S // UNIT
 HALF = S // 2
-VECTOR_SQUARES = (5,)
 
 
 def entries(lst, start, count):
@@ -71,11 +70,12 @@ def tile_picked_candkindgkern_none_po_kernel(
         nc.sync.dma_start(gain[:], gs.rearrange("(p t) o -> p (t o)", t=PACK))
         n1_l = load_list("n1_l", n1)
         tab_rows = tab.rearrange("(p t) c -> p t c", t=PACK)
-        tabs = [sbuf("tab%d" % t, [P, S], F32) for t in range(PACK)]
-        nc.sync.dma_start(tabs[0][:], tab_rows[:, 0, :])
+        score = [sbuf("score%d" % t, [P, 2 * S], F32) for t in range(PACK)]
+        tabs = [score[t][:, S : 2 * S] for t in range(PACK)]
+        nc.sync.dma_start(tabs[0], tab_rows[:, 0, :])
         n2_l = load_list("n2_l", n2)
         for t in range(1, PACK):
-            nc.sync.dma_start(tabs[t][:], tab_rows[:, t, :])
+            nc.sync.dma_start(tabs[t], tab_rows[:, t, :])
         n3_l = load_list("n3_l", n3)
         n4_l = load_list("n4_l", n4)
         ident = sbuf("ident", [P, P], F32)
@@ -104,7 +104,7 @@ def tile_picked_candkindgkern_none_po_kernel(
 
         tab2 = [sbuf("tab2_%d" % t, [P, S], F32) for t in range(PACK)]
         for t in range(PACK):
-            nc.scalar.activation(tab2[t][:], tabs[t][:], ACT.Copy, scale=2.0)
+            nc.scalar.activation(tab2[t][:], tabs[t], ACT.Copy, scale=2.0)
         hy = [sbuf("hy%d" % t, [P, S], F32) for t in range(PACK)]
         ys = [bank(t, "y%d" % t, [P, S]) for t in range(PACK)]
         for t in range(PACK):
@@ -123,33 +123,12 @@ def tile_picked_candkindgkern_none_po_kernel(
             if t > 0:
                 nc.scalar.activation(hy[t - 1][:, HALF:S], ys[t - 1][:, HALF:S], ACT.Copy, scale=half_gain[:, t - 1 : t])
 
-        score = [sbuf("score%d" % t, [P, S], F32) for t in range(PACK)]
-        neg = [sbuf("neg%d" % h, [P, PACK, HALF], F32) for h in range(2)]
+        neg = sbuf("neg", [P, PACK, S], F32)
+        every = range(PACK)
+        num, turned = [], []
 
-        def neg_unit(c):
-            return neg[c // 2][:, :, (c % 2) * UNIT : (c % 2 + 1) * UNIT]
-
-        def quantised(name, z, n, copy, tag):
-            zb = sb.tile([P, n, PACK], BF16, name="zb" + name, tag=tag, align_bytes=64)
-            interleave(copy, zb[:], z[:])
-            z_w = sbuf("z_w" + name, [P, n], U32)
-            z_s = sbuf("z_s" + name, [P, n], U8)
-            nc.vector.quantize_mx(out=z_w[:].bitcast(FP8X4), scales=z_s[:], in_=zb[:].rearrange("p n t -> p (n t)"))
-            return z_w, z_s
-
-        def second_product(dst, t, zq, start, n):
-            nc.tensor.matmul_mx(
-                out=dst,
-                lhsT=cand_w[:, P * t : P * (t + 1)].bitcast(FP8X4),
-                lhsT_scale=cand_sd[:, P * t : P * (t + 1)],
-                rhs=zq[0][:].bitcast(FP8X4),
-                rhs_scale=zq[1][:],
-                start=True,
-                stop=True,
-            )
-
-        def keep_scores(src, t, start, n):
-            nc.scalar.activation(score[t][:, start : start + n], src, ACT.Copy, scale=0.0625)
+        def unit_of(tile, c):
+            return tile[:, :, c * UNIT : (c + 1) * UNIT]
 
         def add_transposed(dst, src, ts, first, last):
             for t in ts:
@@ -157,139 +136,110 @@ def tile_picked_candkindgkern_none_po_kernel(
                     dst[:, t, :], src[:, t, :], ident[:], start=first and t == 0, stop=last and t == PACK - 1, is_transpose=True
                 )
 
-        def unit_of(tile, i):
-            return tile[:, :, i * UNIT : (i + 1) * UNIT]
-
-        every = range(PACK)
-        num, turned = [], []
-
         def turn_scores(c, tag):
             tmp = bank(c, "neg_turned%d" % c, [P, PACK, UNIT])
-            add_transposed(tmp, neg_unit(c), every, True, True)
+            add_transposed(tmp, unit_of(neg, c), every, True, True)
             turned.append(sb.tile([P, PACK, UNIT], F32, name="turned%d" % c, tag=tag, align_bytes=64))
             nc.vector.tensor_scalar_mul(turned[c][:], tmp[:], -1.0)
             acc = bank(c, "num%d" % c, [P, PACK, UNIT])
-            add_transposed(acc, neg_unit(c), every, True, False)
+            add_transposed(acc, unit_of(neg, c), every, True, False)
             num.append(acc)
 
-        def scaled_by_tab(prod, t, start):
-            nc.vector.tensor_tensor(
-                prod, tab2[t][:].indirect(entries(n1_l, start, HALF)), hy[t][:, start : start + HALF], ALU.mult
-            )
-
-        def less_neighbour(z, t, prod, lo, start, n):
-            nc.vector.tensor_tensor(z[:, t, :], hy[t][:].indirect(entries(n2_l, start, n)), prod[:, lo : lo + n], ALU.subtract)
-
-        first_prod = sb.tile([P, PACK, HALF], F32, name="first_prod", tag="prod", align_bytes=64)
-        prod = [first_prod[:, t, :] for t in range(PACK)]
-        z = sbuf("z0", [P, PACK, HALF], F32)
-        for t in range(PACK + 1):
-            if t < PACK:
-                scaled_by_tab(prod[t], t, 0)
-            if t > 0:
-                less_neighbour(z, t - 1, prod[t - 1], 0, 0, HALF)
-        zq = quantised("0", z, HALF, nc.scalar.copy, "rounded")
-        second_prod = sb.tile([P, PACK - 1, HALF], F32, name="second_prod", tag="prod", align_bytes=64)
-        last_prod = sb.tile([P, HALF], F32, name="last_prod", tag="rounded", align_bytes=64)
-        prod = [second_prod[:, t, :] for t in range(PACK - 1)] + [last_prod[:]]
-        for t in range(PACK):
-            scaled_by_tab(prod[t], t, HALF)
-        raw = [bank(4 + b, "raw%d" % b, [P, 2, HALF]) for b in range(2)]
-        for t in range(PACK):
-            second_product(raw[t // 2][:, t % 2, :], t, zq, 0, HALF)
-        for t in range(PACK):
-            keep_scores(raw[t // 2][:, t % 2, :], t, 0, HALF)
-        nc.scalar.activation(neg[0][:, 0:2, :], raw[0][:], ACT.Copy, scale=-0.0625)
-        zs = [sbuf("z%d" % c, [P, PACK, UNIT], F32) for c in (2, 3)]
-        for i in range(2):
-            for t in range(PACK):
-                less_neighbour(zs[i], t, prod[t], i * UNIT, HALF + i * UNIT, UNIT)
-        zq2 = quantised("2", zs[0], UNIT, nc.scalar.copy, "zb2")
-        nc.scalar.activation(neg[0][:, 2:4, :], raw[1][:], ACT.Copy, scale=-0.0625)
-        zq3 = quantised("3", zs[1], UNIT, nc.vector.tensor_copy, "zb3")
-        turn_scores(0, "zb3")
-        for c, zq in ((2, zq2), (3, zq3)):
-            late = bank(4 + c, "raw%d" % c, [P, PACK, UNIT])
-            for t in range(PACK):
-                second_product(late[:, t, :], t, zq, c * UNIT, UNIT)
-            for t in range(PACK):
-                keep_scores(late[:, t, :], t, c * UNIT, UNIT)
-            if c == 2:
-                nc.vector.tensor_scalar_mul(neg_unit(c), late[:], -0.0625)
-            else:
-                nc.scalar.activation(neg_unit(c), late[:], ACT.Copy, scale=-0.0625)
+        for h in range(2):
+            cols = slice(h * HALF, (h + 1) * HALF)
+            prod = sb.tile([P, PACK, HALF], F32, name="prod%d" % h, tag="prod", align_bytes=64)
+            z = sb.tile([P, PACK, HALF], F32, name="z%d" % h, tag="rounded%d" % (1 - h), align_bytes=64)
+            for t in range(PACK + 1):
+                if t < PACK:
+                    nc.vector.tensor_tensor(
+                        prod[:, t, :], tab2[t][:].indirect(entries(n1_l, h * HALF, HALF)), hy[t][:, cols], ALU.mult
+                    )
+                if t > 0:
+                    nc.vector.tensor_tensor(
+                        z[:, t - 1, :], hy[t - 1][:].indirect(entries(n2_l, h * HALF, HALF)), prod[:, t - 1, :], ALU.subtract
+                    )
+            zb = sb.tile([P, HALF, PACK], BF16, name="zb%d" % h, tag="rounded%d" % h, align_bytes=64)
+            interleave(nc.vector.tensor_copy if h else nc.scalar.copy, zb[:], z[:])
+            z_w = sbuf("z_w%d" % h, [P, HALF], U32)
+            z_s = sbuf("z_s%d" % h, [P, HALF], U8)
+            nc.vector.quantize_mx(out=z_w[:].bitcast(FP8X4), scales=z_s[:], in_=zb[:].rearrange("p n t -> p (n t)"))
+            raw = [bank(4 + 2 * h + b, "raw%d_%d" % (h, b), [P, 2, HALF]) for b in range(2)]
+            for t in every:
+                nc.tensor.matmul_mx(
+                    out=raw[t // 2][:, t % 2, :],
+                    lhsT=cand_w[:, P * t : P * (t + 1)].bitcast(FP8X4),
+                    lhsT_scale=cand_sd[:, P * t : P * (t + 1)],
+                    rhs=z_w[:].bitcast(FP8X4),
+                    rhs_scale=z_s[:],
+                    start=True,
+                    stop=True,
+                )
+            for t in every:
+                nc.scalar.activation(score[t][:, cols], raw[t // 2][:, t % 2, :], ACT.Copy, scale=0.0625)
+                if t in (0, 3):
+                    b = t // 2
+                    nc.scalar.activation(neg[:, 2 * b : 2 * b + 2, cols], raw[b][:], ACT.Copy, scale=-0.0625)
+        turn_scores(0, "rounded1")
 
         root = sbuf("root", [P, UNITS, PACK * UNIT], F32)
         wsum = [bank(4 + c, "wsum%d" % c, [P, PACK, UNIT]) for c in range(UNITS)]
-        diff, weight = {}, {}
-        steps = []
-        for h in range(2):
-            for j in range(2):
-                diff[h, j] = sbuf("diff%d_%d" % (h, j), [P, PACK, HALF], F32)
-                weight[h, j] = sbuf("weight%d_%d" % (h, j), [P, PACK, HALF], F32)
-                groups = ((0, 1), (2,), (3,)) if (h, j) == (1, 1) else ((0, 1), (2, 3))
-                steps.extend((h, j, ts) for ts in groups)
-
-        def fetch(h, j, t):
-            nc.vector.tensor_tensor(
-                diff[h, j][:, t, :],
-                score[t][:].indirect(entries((n3_l, n4_l)[j], h * HALF, HALF)),
-                neg[h][:, t, :],
-                ALU.add,
-            )
-
-        def rows_of(tile, ts):
-            flat = tile[:, ts[0] : ts[-1] + 1, :].rearrange("p t n -> p (t n)")
-            return flat.rearrange("p (a b) -> p a b", a=UNITS)
-
+        diff = [sbuf("diff%d" % j, [P, PACK, S], F32) for j in range(2)]
+        weight = [sbuf("weight%d" % j, [P, PACK, S], F32) for j in range(2)]
+        steps = [(j, t, 0, S) for j in range(2) for t in every][:-1] + [(1, PACK - 1, 0, HALF), (1, PACK - 1, HALF, HALF)]
         squares = []
 
+        def fetch(j, t, start, n):
+            cols = slice(start, start + n)
+            nc.vector.tensor_tensor(
+                diff[j][:, t, cols], score[t][:].indirect(entries((n3_l, n4_l)[j], start, n)), neg[:, t, cols], ALU.add
+            )
+
+        def quarters(ap):
+            return ap.rearrange("p (a b) -> p a b", a=UNITS)
+
         def square(k):
-            h, j, ts = steps[k]
+            j, t, start, n = steps[k]
             if k == len(steps) - 1:
-                sq = root[:, :, 0 : HALF // UNITS]
+                sq = root[:, :, 0 : n // UNITS]
             else:
-                sq = sb.tile([P, UNITS, len(ts) * HALF // UNITS], F32, name="sq%d" % k, tag="sq%d" % k, align_bytes=64)[:]
-            d = rows_of(diff[h, j], ts)
-            if k in VECTOR_SQUARES:
+                sq = sb.tile([P, UNITS, n // UNITS], F32, name="sq%d" % k, tag="sq%d" % k, align_bytes=64)[:]
+            d = quarters(diff[j][:, t, start : start + n])
+            if n < S:
                 nc.vector.tensor_tensor(sq, d, d, ALU.mult)
             else:
                 nc.scalar.activation(sq, d, ACT.Square)
             squares.append(sq)
 
         def weigh(k):
-            h, j, ts = steps[k]
-            nc.scalar.activation(rows_of(weight[h, j], ts), squares[k], ACT.Exp, scale=-0.5)
-            for i in range(2):
-                add_transposed(wsum[2 * h + i], unit_of(weight[h, j], i), ts, j == 0, j == 1)
+            j, t, start, n = steps[k]
+            nc.scalar.activation(quarters(weight[j][:, t, start : start + n]), squares[k], ACT.Exp, scale=-0.5)
+            for c in range(start // UNIT, (start + n) // UNIT):
+                add_transposed(wsum[c], unit_of(weight[j], c), (t,), j == 0, j == 1)
 
-        for k, (h, j, ts) in enumerate(steps):
-            fetch(h, j, ts[0])
+        for k, (j, t, start, n) in enumerate(steps):
+            if k == 0:
+                fetch(j, t, 0, HALF)
+                fetch(j, t, HALF, HALF)
+            else:
+                fetch(j, t, start, n)
             if k > 0:
                 square(k - 1)
             if k > 1:
                 weigh(k - 2)
-            for t in ts[1:]:
-                fetch(h, j, t)
         square(len(steps) - 1)
         weigh(len(steps) - 2)
         weigh(len(steps) - 1)
         for c in range(1, UNITS):
             turn_scores(c, "sq%d" % (c + 2))
-        pulls = sb.tile([P, 4, PACK, HALF], F32, name="pulls", tag="sq6", align_bytes=64)
+        pulls = sb.tile([P, 2, PACK, S], F32, name="pulls", tag="sq6", align_bytes=64)
         for h in range(2):
+            cols = slice(h * HALF, (h + 1) * HALF)
             for j in range(2):
-                pull = pulls[:, 2 * h + j, :, :]
                 nc.vector.scalar_tensor_tensor(
-                    pull.rearrange("p t n -> p (t n)"),
-                    weight[h, j][:].rearrange("p t n -> p (t n)"),
-                    2.0,
-                    diff[h, j][:].rearrange("p t n -> p (t n)"),
-                    ALU.mult,
-                    ALU.mult,
+                    pulls[:, j, :, cols], weight[j][:, :, cols], 2.0, diff[j][:, :, cols], ALU.mult, ALU.mult
                 )
-                for i in range(2):
-                    add_transposed(num[2 * h + i], unit_of(pull, i), every, False, j == 1)
+                for c in (2 * h, 2 * h + 1):
+                    add_transposed(num[c], unit_of(pulls[:, j, :, :], c), every, False, j == 1)
 
         out_rows = out_0.rearrange("(p t) j -> p t j", t=PACK)
         words_out = out_1[0].rearrange("p n t -> p (n t)").bitcast(I32)

@@ -3,8 +3,9 @@ from contextlib import ExitStack
 import concourse.mybir as mybir
 from concourse.masks import make_identity
 
-K, T, S = 512, 2048, 512
-FLOPS = 2 * 2 * 512 * 512 * 512
+T = 2048
+S = 512
+FLOPS = 2 * 2 * S * S * S
 
 F32 = mybir.dt.float32
 BF16 = mybir.dt.bfloat16
@@ -19,116 +20,50 @@ ALU = mybir.AluOpType
 
 P = 128
 PACK = 4
+QUADRANTS = 4
+STRIPE = 16
 UNIT = 128
 UNITS = S // UNIT
 HALF = S // 2
+EARLY_TURNS = 2
+SCORE_SCALE = 0.0625
 
 
 def entries(lst, start, count):
-    return lst[:, start // 16 : (start + count) // 16]
+    return lst[:, start // STRIPE : (start + count) // STRIPE]
 
 
 def interleave(copy, dst, src):
     copy(dst.rearrange("p (c i) t -> p c t i", i=4), src.rearrange("p t (c i) -> p c t i", i=4))
 
 
+def unit_of(dealt, c):
+    return dealt[:, :, c * UNIT : (c + 1) * UNIT]
+
+
 def tile_picked_candkindgkern_none_po_kernel(
     tc, x_words, x_scales, w1_words, w1_scales, tab, gs, offs, n1, n2, cand, n3, n4, out_0, out_1, out_2
 ):
     nc = tc.nc
+    slots = range(PACK)
     with ExitStack() as ctx:
         lists = ctx.enter_context(tc.tile_pool(name="lists", bufs=1))
         sb = ctx.enter_context(tc.tile_pool(name="sb", bufs=1))
         psum = ctx.enter_context(tc.psum_pool(name="psum", bufs=1))
 
-        def sbuf(name, shape, dtype):
-            return sb.tile(shape, dtype, name=name, align_bytes=64)
+        def sbuf(name, shape, dtype, tag=None):
+            return sb.tile(shape, dtype, name=name, tag=tag or name, align_bytes=64)
 
         def bank(b, name, shape):
             return psum.tile(shape, F32, name=name, tag="bank%d" % b)
 
         def load_list(name, src):
-            lst = lists.tile([P, S // 16], U16, name=name)
+            lst = lists.tile([P, S // STRIPE], U16, name=name)
             nc.sync.dma_start(lst[:], src)
             return lst
 
-        xs = sbuf("xs", [P, T], U8)
-        nc.gpsimd.memset(xs[:].bitcast(I32), 0)
-        ws = sb.tile([P, S], U8, name="ws", tag="ws_then_cand", align_bytes=64)
-        nc.gpsimd.memset(ws[:].bitcast(I32), 0)
-        ww = sbuf("ww", [P, 2 * S], U8)
-        nc.sync.dma_start(ww[:].bitcast(I32), w1_words[0].bitcast(I32))
-        offs_l = load_list("offs_l", offs)
-        for q in range(4):
-            nc.sync.dma_start(xs[32 * q : 32 * q + 4, :].bitcast(I32), x_scales[0, 4 * q : 4 * q + 4, :].bitcast(I32))
-        cand_l = load_list("cand_l", cand)
-        xw = sbuf("xw", [P, T], I32)
-        nc.sync.dma_start(xw[:], x_words[0].rearrange("p n t -> p (n t)").bitcast(I32))
-        for q in range(4):
-            (nc.gpsimd if q < 3 else nc.sync).dma_start(ws[32 * q : 32 * q + 4, :].bitcast(I32), w1_scales[0, 4 * q : 4 * q + 4, :].bitcast(I32))
-        gain = sbuf("gain", [P, PACK], F32)
-        nc.sync.dma_start(gain[:], gs.rearrange("(p t) o -> p (t o)", t=PACK))
-        n1_l = load_list("n1_l", n1)
-        tab_rows = tab.rearrange("(p t) c -> p t c", t=PACK)
-        score = [sbuf("score%d" % t, [P, 2 * S], F32) for t in range(PACK)]
-        tabs = [score[t][:, S : 2 * S] for t in range(PACK)]
-        nc.sync.dma_start(tabs[0], tab_rows[:, 0, :])
-        n2_l = load_list("n2_l", n2)
-        for t in range(1, PACK):
-            nc.sync.dma_start(tabs[t], tab_rows[:, t, :])
-        n3_l = load_list("n3_l", n3)
-        n4_l = load_list("n4_l", n4)
-        ident = sbuf("ident", [P, P], F32)
-        make_identity(nc, ident[:])
-        half_gain = sbuf("half_gain", [P, PACK], F32)
-        nc.scalar.activation(half_gain[:], gain[:], ACT.Copy, scale=-0.5)
-
-        ww_d = sbuf("ww_d", [P, 2 * S], U8)
-        nc.vector.tensor_copy(
-            ww_d[:].rearrange("p (t m b) -> p t m b", t=PACK, b=2), ww[:].rearrange("p (m t b) -> p t m b", t=PACK, b=2)
-        )
-        tok_s = sbuf("tok_s", [P, S], U8)
-        nc.vector.tensor_copy(tok_s[:], xs[:].indirect(offs_l[:]))
-        cand_s = sbuf("cand_s", [P, S], U8)
-        nc.vector.tensor_copy(cand_s[:], xs[:].indirect(cand_l[:]))
-        cand_sd = sbuf("cand_sd", [P, S], U8)
-        nc.vector.tensor_copy(
-            cand_sd[:].rearrange("p (t m) -> p t m", t=PACK), cand_s[:].rearrange("p (m t) -> p t m", t=PACK)
-        )
-        ws_d = sbuf("ws_d", [P, S], U8)
-        nc.vector.tensor_copy(ws_d[:].rearrange("p (t m) -> p t m", t=PACK), ws[:].rearrange("p (m t) -> p t m", t=PACK))
-        tok_w = sbuf("tok_w", [P, S], U32)
-        nc.vector.tensor_copy(tok_w[:], xw[:].bitcast(U32).indirect(offs_l[:]))
-        cand_w = sb.tile([P, S], U32, name="cand_w", tag="ws_then_cand", align_bytes=64)
-        nc.vector.tensor_copy(cand_w[:].rearrange("p (t m) -> p m t", t=PACK), xw[:].bitcast(U32).indirect(cand_l[:]))
-
-        tab2 = [sbuf("tab2_%d" % t, [P, S], F32) for t in range(PACK)]
-        for t in range(PACK):
-            nc.scalar.activation(tab2[t][:], tabs[t], ACT.Copy, scale=2.0)
-        hy = [sbuf("hy%d" % t, [P, S], F32) for t in range(PACK)]
-        ys = [bank(t, "y%d" % t, [P, S]) for t in range(PACK)]
-        for t in range(PACK):
-            nc.tensor.matmul_mx(
-                out=ys[t][:],
-                lhsT=ww_d[:, 2 * P * t : 2 * P * (t + 1)].bitcast(FP4X4),
-                lhsT_scale=ws_d[:, P * t : P * (t + 1)],
-                rhs=tok_w[:].bitcast(FP8X4),
-                rhs_scale=tok_s[:],
-                start=True,
-                stop=True,
-            )
-        for t in range(PACK + 1):
-            if t < PACK:
-                nc.scalar.activation(hy[t][:, 0:HALF], ys[t][:, 0:HALF], ACT.Copy, scale=half_gain[:, t : t + 1])
-            if t > 0:
-                nc.scalar.activation(hy[t - 1][:, HALF:S], ys[t - 1][:, HALF:S], ACT.Copy, scale=half_gain[:, t - 1 : t])
-
-        neg = sbuf("neg", [P, PACK, S], F32)
-        every = range(PACK)
-        num, turned = [], []
-
-        def unit_of(tile, c):
-            return tile[:, :, c * UNIT : (c + 1) * UNIT]
+        def load_scale_rows(engine, plane, src, q):
+            engine.dma_start(plane[32 * q : 32 * q + 4, :].bitcast(I32), src[0, 4 * q : 4 * q + 4, :].bitcast(I32))
 
         def add_transposed(dst, src, ts, first, last):
             for t in ts:
@@ -136,19 +71,84 @@ def tile_picked_candkindgkern_none_po_kernel(
                     dst[:, t, :], src[:, t, :], ident[:], start=first and t == 0, stop=last and t == PACK - 1, is_transpose=True
                 )
 
-        def turn_scores(c, tag):
-            tmp = bank(c, "neg_turned%d" % c, [P, PACK, UNIT])
-            add_transposed(tmp, unit_of(neg, c), every, True, True)
-            turned.append(sb.tile([P, PACK, UNIT], F32, name="turned%d" % c, tag=tag, align_bytes=64))
-            nc.vector.tensor_scalar_mul(turned[c][:], tmp[:], -1.0)
-            acc = bank(c, "num%d" % c, [P, PACK, UNIT])
-            add_transposed(acc, unit_of(neg, c), every, True, False)
-            num.append(acc)
+        x_plane = sbuf("x_plane", [P, T], U8)
+        nc.gpsimd.memset(x_plane[:].bitcast(I32), 0)
+        w_plane = sbuf("w_plane", [P, S], U8, tag="w_plane_then_cand")
+        nc.gpsimd.memset(w_plane[:].bitcast(I32), 0)
+        w_codes = sbuf("w_codes", [P, 2 * S], U8)
+        nc.sync.dma_start(w_codes[:].bitcast(I32), w1_words[0].bitcast(I32))
+        offs_l = load_list("offs_l", offs)
+        for q in range(QUADRANTS):
+            load_scale_rows(nc.sync, x_plane, x_scales, q)
+        cand_l = load_list("cand_l", cand)
+        x_codes = sbuf("x_codes", [P, T], I32)
+        nc.sync.dma_start(x_codes[:], x_words[0].rearrange("p n t -> p (n t)").bitcast(I32))
+        for q in range(QUADRANTS):
+            load_scale_rows(nc.gpsimd if q < QUADRANTS - 1 else nc.sync, w_plane, w1_scales, q)
+        gain = sbuf("gain", [P, PACK], F32)
+        nc.sync.dma_start(gain[:], gs.rearrange("(p t) o -> p (t o)", t=PACK))
+        n1_l = load_list("n1_l", n1)
+        score = [sbuf("score%d" % t, [P, 2 * S], F32) for t in slots]
+        tab_rows = tab.rearrange("(p t) c -> p t c", t=PACK)
+        nc.sync.dma_start(score[0][:, S : 2 * S], tab_rows[:, 0, :])
+        n2_l = load_list("n2_l", n2)
+        for t in range(1, PACK):
+            nc.sync.dma_start(score[t][:, S : 2 * S], tab_rows[:, t, :])
+        n3_l = load_list("n3_l", n3)
+        n4_l = load_list("n4_l", n4)
+        ident = sbuf("ident", [P, P], F32)
+        make_identity(nc, ident[:])
+        half_gain = sbuf("half_gain", [P, PACK], F32)
+        nc.scalar.activation(half_gain[:], gain[:], ACT.Copy, scale=-0.5)
 
+        w_codes_dealt = sbuf("w_codes_dealt", [P, 2 * S], U8)
+        nc.vector.tensor_copy(
+            w_codes_dealt[:].rearrange("p (t m b) -> p t m b", t=PACK, b=2),
+            w_codes[:].rearrange("p (m t b) -> p t m b", t=PACK, b=2),
+        )
+        tok_plane = sbuf("tok_plane", [P, S], U8)
+        nc.vector.tensor_copy(tok_plane[:], x_plane[:].indirect(offs_l[:]))
+        cand_plane = sbuf("cand_plane", [P, S], U8)
+        nc.vector.tensor_copy(cand_plane[:], x_plane[:].indirect(cand_l[:]))
+        cand_plane_dealt = sbuf("cand_plane_dealt", [P, S], U8)
+        nc.vector.tensor_copy(
+            cand_plane_dealt[:].rearrange("p (t m) -> p t m", t=PACK), cand_plane[:].rearrange("p (m t) -> p t m", t=PACK)
+        )
+        w_plane_dealt = sbuf("w_plane_dealt", [P, S], U8)
+        nc.vector.tensor_copy(
+            w_plane_dealt[:].rearrange("p (t m) -> p t m", t=PACK), w_plane[:].rearrange("p (m t) -> p t m", t=PACK)
+        )
+        tok_codes = sbuf("tok_codes", [P, S], U32)
+        nc.vector.tensor_copy(tok_codes[:], x_codes[:].bitcast(U32).indirect(offs_l[:]))
+        cand_codes = sbuf("cand_codes", [P, S], U32, tag="w_plane_then_cand")
+        nc.vector.tensor_copy(cand_codes[:].rearrange("p (t m) -> p m t", t=PACK), x_codes[:].bitcast(U32).indirect(cand_l[:]))
+
+        tab2 = [sbuf("tab2_%d" % t, [P, S], F32) for t in slots]
+        for t in slots:
+            nc.scalar.activation(tab2[t][:], score[t][:, S : 2 * S], ACT.Copy, scale=2.0)
+        hy = [sbuf("hy%d" % t, [P, S], F32) for t in slots]
+        y = [bank(t, "y%d" % t, [P, S]) for t in slots]
+        for t in slots:
+            nc.tensor.matmul_mx(
+                out=y[t][:],
+                lhsT=w_codes_dealt[:, 2 * P * t : 2 * P * (t + 1)].bitcast(FP4X4),
+                lhsT_scale=w_plane_dealt[:, P * t : P * (t + 1)],
+                rhs=tok_codes[:].bitcast(FP8X4),
+                rhs_scale=tok_plane[:],
+                start=True,
+                stop=True,
+            )
+        for t in range(PACK + 1):
+            if t < PACK:
+                nc.scalar.activation(hy[t][:, 0:HALF], y[t][:, 0:HALF], ACT.Copy, scale=half_gain[:, t : t + 1])
+            if t > 0:
+                nc.scalar.activation(hy[t - 1][:, HALF:S], y[t - 1][:, HALF:S], ACT.Copy, scale=half_gain[:, t - 1 : t])
+
+        neg = sbuf("neg", [P, PACK, S], F32)
         for h in range(2):
             cols = slice(h * HALF, (h + 1) * HALF)
-            prod = sb.tile([P, PACK, HALF], F32, name="prod%d" % h, tag="prod", align_bytes=64)
-            z = sb.tile([P, PACK, HALF], F32, name="z%d" % h, tag="rounded%d" % (1 - h), align_bytes=64)
+            prod = sbuf("prod%d" % h, [P, PACK, HALF], F32, tag="prod")
+            z = sbuf("z%d" % h, [P, PACK, HALF], F32, tag="z_stage%d" % (1 - h))
             for t in range(PACK + 1):
                 if t < PACK:
                     nc.vector.tensor_tensor(
@@ -158,51 +158,69 @@ def tile_picked_candkindgkern_none_po_kernel(
                     nc.vector.tensor_tensor(
                         z[:, t - 1, :], hy[t - 1][:].indirect(entries(n2_l, h * HALF, HALF)), prod[:, t - 1, :], ALU.subtract
                     )
-            zb = sb.tile([P, HALF, PACK], BF16, name="zb%d" % h, tag="rounded%d" % h, align_bytes=64)
-            interleave(nc.vector.tensor_copy if h else nc.scalar.copy, zb[:], z[:])
-            z_w = sbuf("z_w%d" % h, [P, HALF], U32)
-            z_s = sbuf("z_s%d" % h, [P, HALF], U8)
-            nc.vector.quantize_mx(out=z_w[:].bitcast(FP8X4), scales=z_s[:], in_=zb[:].rearrange("p n t -> p (n t)"))
-            raw = [bank(4 + 2 * h + b, "raw%d_%d" % (h, b), [P, 2, HALF]) for b in range(2)]
-            for t in every:
+            z_rounded = sbuf("z_rounded%d" % h, [P, HALF, PACK], BF16, tag="z_stage%d" % h)
+            interleave(nc.vector.tensor_copy if h else nc.scalar.copy, z_rounded[:], z[:])
+            z_codes = sbuf("z_codes%d" % h, [P, HALF], U32)
+            z_plane = sbuf("z_plane%d" % h, [P, HALF], U8)
+            nc.vector.quantize_mx(
+                out=z_codes[:].bitcast(FP8X4), scales=z_plane[:], in_=z_rounded[:].rearrange("p n t -> p (n t)")
+            )
+            raw = [bank(PACK + 2 * h + b, "raw%d_%d" % (h, b), [P, 2, HALF]) for b in range(2)]
+            for t in slots:
                 nc.tensor.matmul_mx(
                     out=raw[t // 2][:, t % 2, :],
-                    lhsT=cand_w[:, P * t : P * (t + 1)].bitcast(FP8X4),
-                    lhsT_scale=cand_sd[:, P * t : P * (t + 1)],
-                    rhs=z_w[:].bitcast(FP8X4),
-                    rhs_scale=z_s[:],
+                    lhsT=cand_codes[:, P * t : P * (t + 1)].bitcast(FP8X4),
+                    lhsT_scale=cand_plane_dealt[:, P * t : P * (t + 1)],
+                    rhs=z_codes[:].bitcast(FP8X4),
+                    rhs_scale=z_plane[:],
                     start=True,
                     stop=True,
                 )
-            for t in every:
-                nc.scalar.activation(score[t][:, cols], raw[t // 2][:, t % 2, :], ACT.Copy, scale=0.0625)
-                if t in (0, 3):
+            for t in slots:
+                nc.scalar.activation(score[t][:, cols], raw[t // 2][:, t % 2, :], ACT.Copy, scale=SCORE_SCALE)
+                if t in (0, PACK - 1):
                     b = t // 2
-                    nc.scalar.activation(neg[:, 2 * b : 2 * b + 2, cols], raw[b][:], ACT.Copy, scale=-0.0625)
-        turn_scores(0, "rounded1")
+                    nc.scalar.activation(neg[:, 2 * b : 2 * b + 2, cols], raw[b][:], ACT.Copy, scale=-SCORE_SCALE)
 
-        root = sbuf("root", [P, UNITS, PACK * UNIT], F32)
-        wsum = [bank(4 + c, "wsum%d" % c, [P, PACK, UNIT]) for c in range(UNITS)]
+        numer, turned = [], []
+
+        def turn_scores(c, dst):
+            neg_turned = bank(c, "neg_turned%d" % c, [P, PACK, UNIT])
+            add_transposed(neg_turned, unit_of(neg, c), slots, True, True)
+            nc.vector.tensor_scalar_mul(dst, neg_turned[:], -1.0)
+            turned.append(dst)
+            numer.append(bank(c, "numer%d" % c, [P, PACK, UNIT]))
+            add_transposed(numer[c], unit_of(neg, c), slots, True, False)
+
+        turned_early = sbuf("turned_early", [P, EARLY_TURNS, PACK, UNIT], F32, tag="z_stage1")
+        for c in range(EARLY_TURNS):
+            turn_scores(c, turned_early[:, c, :, :])
+
+        log_den = sbuf("log_den", [P, UNITS, PACK * UNIT], F32)
+        weight_sum = [bank(PACK + c, "weight_sum%d" % c, [P, PACK, UNIT]) for c in range(UNITS)]
         diff = [sbuf("diff%d" % j, [P, PACK, S], F32) for j in range(2)]
         weight = [sbuf("weight%d" % j, [P, PACK, S], F32) for j in range(2)]
-        steps = [(j, t, 0, S) for j in range(2) for t in every][:-1] + [(1, PACK - 1, 0, HALF), (1, PACK - 1, HALF, HALF)]
+        steps = [(j, t, 0, S) for j in range(2) for t in slots][:-1] + [(1, PACK - 1, 0, HALF), (1, PACK - 1, HALF, HALF)]
+        last = len(steps) - 1
         squares = []
 
         def fetch(j, t, start, n):
-            cols = slice(start, start + n)
             nc.vector.tensor_tensor(
-                diff[j][:, t, cols], score[t][:].indirect(entries((n3_l, n4_l)[j], start, n)), neg[:, t, cols], ALU.add
+                diff[j][:, t, start : start + n],
+                score[t][:].indirect(entries((n3_l, n4_l)[j], start, n)),
+                neg[:, t, start : start + n],
+                ALU.add,
             )
 
-        def quarters(ap):
-            return ap.rearrange("p (a b) -> p a b", a=UNITS)
+        def quarters(row):
+            return row.rearrange("p (a b) -> p a b", a=UNITS)
 
         def square(k):
             j, t, start, n = steps[k]
-            if k == len(steps) - 1:
-                sq = root[:, :, 0 : n // UNITS]
+            if k == last:
+                sq = log_den[:, :, 0 : n // UNITS]
             else:
-                sq = sb.tile([P, UNITS, n // UNITS], F32, name="sq%d" % k, tag="sq%d" % k, align_bytes=64)[:]
+                sq = sbuf("square%d" % k, [P, UNITS, n // UNITS], F32)[:]
             d = quarters(diff[j][:, t, start : start + n])
             if n < S:
                 nc.vector.tensor_tensor(sq, d, d, ALU.mult)
@@ -214,62 +232,60 @@ def tile_picked_candkindgkern_none_po_kernel(
             j, t, start, n = steps[k]
             nc.scalar.activation(quarters(weight[j][:, t, start : start + n]), squares[k], ACT.Exp, scale=-0.5)
             for c in range(start // UNIT, (start + n) // UNIT):
-                add_transposed(wsum[c], unit_of(weight[j], c), (t,), j == 0, j == 1)
+                add_transposed(weight_sum[c], unit_of(weight[j], c), (t,), j == 0, j == 1)
 
-        for k, (j, t, start, n) in enumerate(steps):
-            if k == 0:
-                fetch(j, t, 0, HALF)
-                fetch(j, t, HALF, HALF)
-            else:
-                fetch(j, t, start, n)
-            if k > 0:
+        fetch(0, 0, 0, HALF)
+        fetch(0, 0, HALF, HALF)
+        for k in range(1, last + 3):
+            if k <= last:
+                fetch(*steps[k])
+            if k - 1 <= last:
                 square(k - 1)
-            if k > 1:
+            if k >= 2:
                 weigh(k - 2)
-        square(len(steps) - 1)
-        weigh(len(steps) - 2)
-        weigh(len(steps) - 1)
-        for c in range(1, UNITS):
-            turn_scores(c, "sq%d" % (c + 2))
-        pulls = sb.tile([P, 2, PACK, S], F32, name="pulls", tag="sq6", align_bytes=64)
+
+        turned_late = sbuf("turned_late", [P, UNITS - EARLY_TURNS, PACK, UNIT], F32, tag="square%d" % (last - 2))
+        for c in range(EARLY_TURNS, UNITS):
+            turn_scores(c, turned_late[:, c - EARLY_TURNS, :, :])
+        pull = sbuf("pull", [P, 2, PACK, S], F32, tag="square%d" % (last - 1))
         for h in range(2):
             cols = slice(h * HALF, (h + 1) * HALF)
             for j in range(2):
                 nc.vector.scalar_tensor_tensor(
-                    pulls[:, j, :, cols], weight[j][:, :, cols], 2.0, diff[j][:, :, cols], ALU.mult, ALU.mult
+                    pull[:, j, :, cols], weight[j][:, :, cols], 2.0, diff[j][:, :, cols], ALU.mult, ALU.mult
                 )
                 for c in (2 * h, 2 * h + 1):
-                    add_transposed(num[c], unit_of(pulls[:, j, :, :], c), every, False, j == 1)
+                    add_transposed(numer[c], unit_of(pull[:, j, :, :], c), slots, False, j == 1)
 
-        out_rows = out_0.rearrange("(p t) j -> p t j", t=PACK)
-        words_out = out_1[0].rearrange("p n t -> p (n t)").bitcast(I32)
-        o_w = sbuf("o_w", [P, S], U32)
-        o_s = sbuf("o_s", [P, S], U8)
         recip = [sbuf("recip%d" % c, [P, PACK * UNIT], F32) for c in range(UNITS)]
         for c in range(UNITS):
-            nc.scalar.activation(
-                root[:, c, :], wsum[c][:].rearrange("p t n -> p (t n)"), ACT.Ln, scale=2.0, bias=1.0
-            )
+            nc.scalar.activation(log_den[:, c, :], weight_sum[c][:].rearrange("p t n -> p (t n)"), ACT.Ln, scale=2.0, bias=1.0)
         for c in range(UNITS):
-            nc.scalar.activation(recip[c][:], root[:, c, :], ACT.Exp, scale=-1.0)
-        back = [bank(4 + c, "back%d" % c, [P, PACK, UNIT]) for c in range(UNITS)]
+            nc.scalar.activation(recip[c][:], log_den[:, c, :], ACT.Exp, scale=-1.0)
+        result = [bank(PACK + c, "result%d" % c, [P, PACK, UNIT]) for c in range(UNITS)]
         for c in range(UNITS):
-            add_transposed(back[c], turned[c], every, True, False)
+            add_transposed(result[c], turned[c], slots, True, False)
         for c in range(UNITS):
-            shift = sbuf("shift%d" % c, [P, PACK, UNIT], F32)
+            quotient = sbuf("quotient%d" % c, [P, PACK, UNIT], F32)
             nc.vector.tensor_tensor(
-                shift[:].rearrange("p t n -> p (t n)"), num[c][:].rearrange("p t n -> p (t n)"), recip[c][:], ALU.mult
+                quotient[:].rearrange("p t n -> p (t n)"), numer[c][:].rearrange("p t n -> p (t n)"), recip[c][:], ALU.mult
             )
-            add_transposed(back[c], shift, every, False, True)
+            add_transposed(result[c], quotient, slots, False, True)
+        out_rows = out_0.rearrange("(p t) j -> p t j", t=PACK)
+        out_words = out_1[0].rearrange("p n t -> p (n t)").bitcast(I32)
+        out_codes = sbuf("out_codes", [P, S], U32)
+        out_plane = sbuf("out_plane", [P, S], U8)
         for c in range(UNITS):
             cols = slice(c * UNIT, (c + 1) * UNIT)
-            res = sbuf("res%d" % c, [P, PACK, UNIT], F32)
-            rb = sbuf("rb%d" % c, [P, UNIT, PACK], BF16)
-            nc.scalar.copy(res[:], back[c][:])
-            nc.sync.dma_start(out_rows[:, :, cols], res[:])
-            interleave(nc.vector.tensor_copy, rb[:], res[:])
-            nc.vector.quantize_mx(out=o_w[:, cols].bitcast(FP8X4), scales=o_s[:, cols], in_=rb[:].rearrange("p n t -> p (n t)"))
-            nc.sync.dma_start(words_out[:, cols], o_w[:, cols].bitcast(I32))
-        for q in range(4):
-            eng = nc.scalar if q % 2 else nc.sync
-            eng.dma_start(out_2[0, 4 * q : 4 * q + 4, :].bitcast(I32), o_s[32 * q : 32 * q + 4, :].bitcast(I32))
+            values = sbuf("values%d" % c, [P, PACK, UNIT], F32)
+            nc.scalar.copy(values[:], result[c][:])
+            nc.sync.dma_start(out_rows[:, :, cols], values[:])
+            rounded = sbuf("rounded%d" % c, [P, UNIT, PACK], BF16)
+            interleave(nc.vector.tensor_copy, rounded[:], values[:])
+            nc.vector.quantize_mx(
+                out=out_codes[:, cols].bitcast(FP8X4), scales=out_plane[:, cols], in_=rounded[:].rearrange("p n t -> p (n t)")
+            )
+            nc.sync.dma_start(out_words[:, cols], out_codes[:, cols].bitcast(I32))
+        for q in range(QUADRANTS):
+            engine = nc.scalar if q % 2 else nc.sync
+            engine.dma_start(out_2[0, 4 * q : 4 * q + 4, :].bitcast(I32), out_plane[32 * q : 32 * q + 4, :].bitcast(I32))

@@ -96,16 +96,16 @@ def tile_picked_candkindgkern_none_po_kernel(
             nc.sync.dma_start(score[t][:, S : 2 * S], tab_rows[:, t, :])
         n3_l = load_list("n3_l", n3)
         n4_l = load_list("n4_l", n4)
-        ident = sbuf("ident", [P, P], F32)
-        make_identity(nc, ident[:])
         half_gain = sbuf("half_gain", [P, PACK], F32)
         nc.scalar.activation(half_gain[:], gain[:], ACT.Copy, scale=-0.5)
 
         w_codes_dealt = sbuf("w_codes_dealt", [P, 2 * S], U8)
-        nc.vector.tensor_copy(
+        nc.gpsimd.tensor_copy(
             w_codes_dealt[:].rearrange("p (t m b) -> p t m b", t=PACK, b=2),
             w_codes[:].rearrange("p (m t b) -> p t m b", t=PACK, b=2),
         )
+        ident = sbuf("ident", [P, P], F32)
+        make_identity(nc, ident[:])
         tok_plane = sbuf("tok_plane", [P, S], U8)
         nc.vector.tensor_copy(tok_plane[:], x_plane[:].indirect(offs_l[:]))
         cand_plane = sbuf("cand_plane", [P, S], U8)

from contextlib import ExitStack

import concourse.mybir as mybir
from concourse.masks import make_identity

T = 2048
S = 512
FLOPS = 2 * 2 * S * S * S

F32 = mybir.dt.float32
BF16 = mybir.dt.bfloat16
I32 = mybir.dt.int32
U32 = mybir.dt.uint32
U16 = mybir.dt.uint16
U8 = mybir.dt.uint8
FP8X4 = mybir.dt.float8_e4m3fn_x4
FP4X4 = mybir.dt.float4_e2m1fn_x4
ACT = mybir.ActivationFunctionType
ALU = mybir.AluOpType

P = 128
PACK = 4
QUADRANTS = 4
STRIPE = 16
UNIT = 128
UNITS = S // UNIT
HALF = S // 2
EARLY_TURNS = 2
SCORE_SCALE = 0.0625


def entries(lst, start, count):
    return lst[:, start // STRIPE : (start + count) // STRIPE]


def interleave(copy, dst, src):
    copy(dst.rearrange("p (c i) t -> p c t i", i=4), src.rearrange("p t (c i) -> p c t i", i=4))


def unit_of(dealt, c):
    return dealt[:, :, c * UNIT : (c + 1) * UNIT]


def tile_picked_candkindgkern_none_po_kernel(
    tc, x_words, x_scales, w1_words, w1_scales, tab, gs, offs, n1, n2, cand, n3, n4, out_0, out_1, out_2
):
    nc = tc.nc
    slots = range(PACK)
    with ExitStack() as ctx:
        lists = ctx.enter_context(tc.tile_pool(name="lists", bufs=1))
        sb = ctx.enter_context(tc.tile_pool(name="sb", bufs=1))
        psum = ctx.enter_context(tc.psum_pool(name="psum", bufs=1))

        def sbuf(name, shape, dtype, tag=None):
            return sb.tile(shape, dtype, name=name, tag=tag or name, align_bytes=64)

        def bank(b, name, shape):
            return psum.tile(shape, F32, name=name, tag="bank%d" % b)

        def load_list(name, src):
            lst = lists.tile([P, S // STRIPE], U16, name=name)
            nc.sync.dma_start(lst[:], src)
            return lst

        def load_scale_rows(engine, plane, src, q):
            engine.dma_start(plane[32 * q : 32 * q + 4, :].bitcast(I32), src[0, 4 * q : 4 * q + 4, :].bitcast(I32))

        def add_transposed(dst, src, ts, first, last):
            for t in ts:
                nc.tensor.matmul(
                    dst[:, t, :], src[:, t, :], ident[:], start=first and t == 0, stop=last and t == PACK - 1, is_transpose=True
                )

        x_plane = sbuf("x_plane", [P, T], U8)
        nc.gpsimd.memset(x_plane[:].bitcast(I32), 0)
        w_plane = sbuf("w_plane", [P, S], U8, tag="w_plane_then_cand")
        nc.gpsimd.memset(w_plane[:].bitcast(I32), 0)
        w_codes = sbuf("w_codes", [P, 2 * S], U8)
        nc.sync.dma_start(w_codes[:].bitcast(I32), w1_words[0].bitcast(I32))
        offs_l = load_list("offs_l", offs)
        for q in range(QUADRANTS):
            load_scale_rows(nc.sync, x_plane, x_scales, q)
        cand_l = load_list("cand_l", cand)
        x_codes = sbuf("x_codes", [P, T], I32)
        nc.sync.dma_start(x_codes[:], x_words[0].rearrange("p n t -> p (n t)").bitcast(I32))
        for q in range(QUADRANTS):
            load_scale_rows(nc.gpsimd if q < QUADRANTS - 1 else nc.sync, w_plane, w1_scales, q)
        gain = sbuf("gain", [P, PACK], F32)
        nc.sync.dma_start(gain[:], gs.rearrange("(p t) o -> p (t o)", t=PACK))
        n1_l = load_list("n1_l", n1)
        score = [sbuf("score%d" % t, [P, 2 * S], F32) for t in slots]
        tab_rows = tab.rearrange("(p t) c -> p t c", t=PACK)
        nc.sync.dma_start(score[0][:, S : 2 * S], tab_rows[:, 0, :])
        n2_l = load_list("n2_l", n2)
        for t in range(1, PACK):
            nc.sync.dma_start(score[t][:, S : 2 * S], tab_rows[:, t, :])
        n3_l = load_list("n3_l", n3)
        n4_l = load_list("n4_l", n4)
        half_gain = sbuf("half_gain", [P, PACK], F32)
        nc.scalar.activation(half_gain[:], gain[:], ACT.Copy, scale=-0.5)

        w_codes_dealt = sbuf("w_codes_dealt", [P, 2 * S], U8)
        nc.gpsimd.tensor_copy(
            w_codes_dealt[:].rearrange("p (t m b) -> p t m b", t=PACK, b=2),
            w_codes[:].rearrange("p (m t b) -> p t m b", t=PACK, b=2),
        )
        ident = sbuf("ident", [P, P], F32)
        make_identity(nc, ident[:])
        tok_plane = sbuf("tok_plane", [P, S], U8)
        nc.vector.tensor_copy(tok_plane[:], x_plane[:].indirect(offs_l[:]))
        cand_plane = sbuf("cand_plane", [P, S], U8)
        nc.vector.tensor_copy(cand_plane[:], x_plane[:].indirect(cand_l[:]))
        cand_plane_dealt = sbuf("cand_plane_dealt", [P, S], U8)
        nc.vector.tensor_copy(
            cand_plane_dealt[:].rearrange("p (t m) -> p t m", t=PACK), cand_plane[:].rearrange("p (m t) -> p t m", t=PACK)
        )
        w_plane_dealt = sbuf("w_plane_dealt", [P, S], U8)
        nc.vector.tensor_copy(
            w_plane_dealt[:].rearrange("p (t m) -> p t m", t=PACK), w_plane[:].rearrange("p (m t) -> p t m", t=PACK)
        )
        tok_codes = sbuf("tok_codes", [P, S], U32)
        nc.vector.tensor_copy(tok_codes[:], x_codes[:].bitcast(U32).indirect(offs_l[:]))
        cand_codes = sbuf("cand_codes", [P, S], U32, tag="w_plane_then_cand")
        nc.vector.tensor_copy(cand_codes[:].rearrange("p (t m) -> p m t", t=PACK), x_codes[:].bitcast(U32).indirect(cand_l[:]))

        tab2 = [sbuf("tab2_%d" % t, [P, S], F32) for t in slots]
        for t in slots:
            nc.scalar.activation(tab2[t][:], score[t][:, S : 2 * S], ACT.Copy, scale=2.0)
        hy = [sbuf("hy%d" % t, [P, S], F32) for t in slots]
        y = [bank(t, "y%d" % t, [P, S]) for t in slots]
        for t in slots:
            nc.tensor.matmul_mx(
                out=y[t][:],
                lhsT=w_codes_dealt[:, 2 * P * t : 2 * P * (t + 1)].bitcast(FP4X4),
                lhsT_scale=w_plane_dealt[:, P * t : P * (t + 1)],
                rhs=tok_codes[:].bitcast(FP8X4),
                rhs_scale=tok_plane[:],
                start=True,
                stop=True,
            )
        for t in range(PACK + 1):
            if t < PACK:
                nc.scalar.activation(hy[t][:, 0:HALF], y[t][:, 0:HALF], ACT.Copy, scale=half_gain[:, t : t + 1])
            if t > 0:
                nc.scalar.activation(hy[t - 1][:, HALF:S], y[t - 1][:, HALF:S], ACT.Copy, scale=half_gain[:, t - 1 : t])

        neg = sbuf("neg", [P, PACK, S], F32)
        for h in range(2):
            cols = slice(h * HALF, (h + 1) * HALF)
            prod = sbuf("prod%d" % h, [P, PACK, HALF], F32, tag="prod")
            z = sbuf("z%d" % h, [P, PACK, HALF], F32, tag="z_stage%d" % (1 - h))
            for t in range(PACK + 1):
                if t < PACK:
                    nc.vector.tensor_tensor(
                        prod[:, t, :], tab2[t][:].indirect(entries(n1_l, h * HALF, HALF)), hy[t][:, cols], ALU.mult
                    )
                if t > 0:
                    nc.vector.tensor_tensor(
                        z[:, t - 1, :], hy[t - 1][:].indirect(entries(n2_l, h * HALF, HALF)), prod[:, t - 1, :], ALU.subtract
                    )
            z_rounded = sbuf("z_rounded%d" % h, [P, HALF, PACK], BF16, tag="z_stage%d" % h)
            interleave(nc.vector.tensor_copy if h else nc.scalar.copy, z_rounded[:], z[:])
            z_codes = sbuf("z_codes%d" % h, [P, HALF], U32)
            z_plane = sbuf("z_plane%d" % h, [P, HALF], U8)
            nc.vector.quantize_mx(
                out=z_codes[:].bitcast(FP8X4), scales=z_plane[:], in_=z_rounded[:].rearrange("p n t -> p (n t)")
            )
            raw = [bank(PACK + 2 * h + b, "raw%d_%d" % (h, b), [P, 2, HALF]) for b in range(2)]
            for t in slots:
                nc.tensor.matmul_mx(
                    out=raw[t // 2][:, t % 2, :],
                    lhsT=cand_codes[:, P * t : P * (t + 1)].bitcast(FP8X4),
                    lhsT_scale=cand_plane_dealt[:, P * t : P * (t + 1)],
                    rhs=z_codes[:].bitcast(FP8X4),
                    rhs_scale=z_plane[:],
                    start=True,
                    stop=True,
                )
            for t in slots:
                nc.scalar.activation(score[t][:, cols], raw[t // 2][:, t % 2, :], ACT.Copy, scale=SCORE_SCALE)
                if t in (0, PACK - 1):
                    b = t // 2
                    nc.scalar.activation(neg[:, 2 * b : 2 * b + 2, cols], raw[b][:], ACT.Copy, scale=-SCORE_SCALE)

        numer, turned = [], []

        def turn_scores(c, dst):
            neg_turned = bank(c, "neg_turned%d" % c, [P, PACK, UNIT])
            add_transposed(neg_turned, unit_of(neg, c), slots, True, True)
            nc.vector.tensor_scalar_mul(dst, neg_turned[:], -1.0)
            turned.append(dst)
            numer.append(bank(c, "numer%d" % c, [P, PACK, UNIT]))
            add_transposed(numer[c], unit_of(neg, c), slots, True, False)

        turned_early = sbuf("turned_early", [P, EARLY_TURNS, PACK, UNIT], F32, tag="z_stage1")
        for c in range(EARLY_TURNS):
            turn_scores(c, turned_early[:, c, :, :])

        log_den = sbuf("log_den", [P, UNITS, PACK * UNIT], F32)
        weight_sum = [bank(PACK + c, "weight_sum%d" % c, [P, PACK, UNIT]) for c in range(UNITS)]
        diff = [sbuf("diff%d" % j, [P, PACK, S], F32) for j in range(2)]
        weight = [sbuf("weight%d" % j, [P, PACK, S], F32) for j in range(2)]
        steps = [(j, t, 0, S) for j in range(2) for t in slots][:-1] + [(1, PACK - 1, 0, HALF), (1, PACK - 1, HALF, HALF)]
        last = len(steps) - 1
        squares = []

        def fetch(j, t, start, n):
            nc.vector.tensor_tensor(
                diff[j][:, t, start : start + n],
                score[t][:].indirect(entries((n3_l, n4_l)[j], start, n)),
                neg[:, t, start : start + n],
                ALU.add,
            )

        def quarters(row):
            return row.rearrange("p (a b) -> p a b", a=UNITS)

        def square(k):
            j, t, start, n = steps[k]
            if k == last:
                sq = log_den[:, :, 0 : n // UNITS]
            else:
                sq = sbuf("square%d" % k, [P, UNITS, n // UNITS], F32)[:]
            d = quarters(diff[j][:, t, start : start + n])
            if n < S:
                nc.vector.tensor_tensor(sq, d, d, ALU.mult)
            else:
                nc.scalar.activation(sq, d, ACT.Square)
            squares.append(sq)

        def weigh(k):
            j, t, start, n = steps[k]
            nc.scalar.activation(quarters(weight[j][:, t, start : start + n]), squares[k], ACT.Exp, scale=-0.5)
            for c in range(start // UNIT, (start + n) // UNIT):
                add_transposed(weight_sum[c], unit_of(weight[j], c), (t,), j == 0, j == 1)

        fetch(0, 0, 0, HALF)
        fetch(0, 0, HALF, HALF)
        for k in range(1, last + 3):
            if k <= last:
                fetch(*steps[k])
            if k - 1 <= last:
                square(k - 1)
            if k >= 2:
                weigh(k - 2)

        turned_late = sbuf("turned_late", [P, UNITS - EARLY_TURNS, PACK, UNIT], F32, tag="square%d" % (last - 2))
        for c in range(EARLY_TURNS, UNITS):
            turn_scores(c, turned_late[:, c - EARLY_TURNS, :, :])
        pull = sbuf("pull", [P, 2, PACK, S], F32, tag="square%d" % (last - 1))
        for h in range(2):
            cols = slice(h * HALF, (h + 1) * HALF)
            for j in range(2):
                nc.vector.scalar_tensor_tensor(
                    pull[:, j, :, cols], weight[j][:, :, cols], 2.0, diff[j][:, :, cols], ALU.mult, ALU.mult
                )
                for c in (2 * h, 2 * h + 1):
                    add_transposed(numer[c], unit_of(pull[:, j, :, :], c), slots, False, j == 1)

        recip = [sbuf("recip%d" % c, [P, PACK * UNIT], F32) for c in range(UNITS)]
        for c in range(UNITS):
            nc.scalar.activation(log_den[:, c, :], weight_sum[c][:].rearrange("p t n -> p (t n)"), ACT.Ln, scale=2.0, bias=1.0)
        for c in range(UNITS):
            nc.scalar.activation(recip[c][:], log_den[:, c, :], ACT.Exp, scale=-1.0)
        result = [bank(PACK + c, "result%d" % c, [P, PACK, UNIT]) for c in range(UNITS)]
        for c in range(UNITS):
            add_transposed(result[c], turned[c], slots, True, False)
        for c in range(UNITS):
            quotient = sbuf("quotient%d" % c, [P, PACK, UNIT], F32)
            nc.vector.tensor_tensor(
                quotient[:].rearrange("p t n -> p (t n)"), numer[c][:].rearrange("p t n -> p (t n)"), recip[c][:], ALU.mult
            )
            add_transposed(result[c], quotient, slots, False, True)
        out_rows = out_0.rearrange("(p t) j -> p t j", t=PACK)
        out_words = out_1[0].rearrange("p n t -> p (n t)").bitcast(I32)
        out_codes = sbuf("out_codes", [P, S], U32)
        out_plane = sbuf("out_plane", [P, S], U8)
        for c in range(UNITS):
            cols = slice(c * UNIT, (c + 1) * UNIT)
            values = sbuf("values%d" % c, [P, PACK, UNIT], F32)
            nc.scalar.copy(values[:], result[c][:])
            nc.sync.dma_start(out_rows[:, :, cols], values[:])
            rounded = sbuf("rounded%d" % c, [P, UNIT, PACK], BF16)
            interleave(nc.vector.tensor_copy, rounded[:], values[:])
            nc.vector.quantize_mx(
                out=out_codes[:, cols].bitcast(FP8X4), scales=out_plane[:, cols], in_=rounded[:].rearrange("p n t -> p (n t)")
            )
            nc.sync.dma_start(out_words[:, cols], out_codes[:, cols].bitcast(I32))
        for q in range(QUADRANTS):
            engine = nc.scalar if q % 2 else nc.sync
            engine.dma_start(out_2[0, 4 * q : 4 * q + 4, :].bitcast(I32), out_plane[32 * q : 32 * q + 4, :].bitcast(I32))
